import numpy as np
import ml_dtypes


def mxq(x, axis, fmt="e4m3"):
    dtype, down = {"e4m3": (ml_dtypes.float8_e4m3fn, 7), "e5m2": (ml_dtypes.float8_e5m2, 14)}[fmt]
    v = np.moveaxis(np.asarray(x, np.float32).astype(ml_dtypes.bfloat16).astype(np.float64), axis, -1)
    blocks = v.reshape(v.shape[:-1] + (-1, 32))
    amax = np.abs(blocks).max(-1, keepdims=True)
    byte = np.maximum(np.where(amax > 0, np.frexp(amax)[1] - 1 + 127, 0) - down, 1)
    scale = np.exp2(byte - 127.0)
    codes = (blocks / scale).astype(np.float32).astype(dtype).astype(np.float64)
    return np.moveaxis((codes * scale).reshape(v.shape), -1, axis)


WIDE = False


def mx_kscale(k):
    if not WIDE:
        return np.ones(k)
    levels = np.array([10, -10, 5, -5, 0])
    if k % 512:
        return np.exp2(np.random.permutation(np.resize(levels, k // 32))).repeat(32)
    a = np.empty((k // 512, 16))
    for p in range(k // 512):
        a[p, :8] = np.random.permutation(np.resize(levels, 8))
        for g in range(8):
            far = levels[np.abs(levels - a[p, g]) >= 10]
            a[p, g + 8] = far[np.random.randint(len(far))]
    return np.exp2(a.ravel()).repeat(32)


def f64(x):
    return np.asarray(x).astype(np.float64)


def striped(idx):
    return np.tile(idx.reshape(-1, 16).T, (8, 1)).astype(np.uint16)


def unstriped(offs):
    return offs[:16].T.reshape(-1).astype(np.int64)


E2M1 = np.array([0.0, 0.5, 1.0, 1.5, 2.0, 3.0, 4.0, 6.0, -0.0, -0.5, -1.0, -1.5, -2.0, -3.0, -4.0, -6.0])


def pack_weight(w, fmt):
    k, n = w.shape
    w = f64(np.asarray(w, np.float32).astype(ml_dtypes.bfloat16)).reshape(k // 32, 32, n)
    amax = np.abs(w).max(1)
    if fmt == "e4m3":
        byte = np.frexp(amax)[1] - 1 + 127 - 7
    else:
        mant, ex = np.frexp(amax / 6.0)
        byte = np.where(mant > 0.5, ex, ex - 1) + 127
    byte = np.clip(np.where(amax > 0, byte, 1), 1, 254)
    scaled = (w * np.exp2(127.0 - byte)[:, None, :]).reshape(k, n).astype(np.float32)
    by_word = np.ascontiguousarray(scaled.reshape(k // 512, 128, 4, n).transpose(0, 1, 3, 2))
    if fmt == "e4m3":
        words = by_word.astype(ml_dtypes.float8_e4m3fn).view(np.uint8)
    else:
        c = by_word.astype(ml_dtypes.float4_e2m1fn).view(np.uint8) & 0xF
        words = (c[..., 0::2] | (c[..., 1::2] << 4)).reshape(k // 512, 128, 2 * n)
    return np.ascontiguousarray(words), np.ascontiguousarray(byte.astype(np.uint8).reshape(k // 512, 16, n))


def unpack_weight(words, scales, fmt):
    g, _, n = scales.shape
    words = np.ascontiguousarray(words).reshape(g, 128, n, -1)
    if fmt == "e4m3":
        vals = words.view(ml_dtypes.float8_e4m3fn).astype(np.float64)
    else:
        nib = np.empty((g, 128, n, 4), np.uint8)
        nib[..., 0::2] = words & 0xF
        nib[..., 1::2] = words >> 4
        vals = E2M1[nib]
    vals = vals * np.repeat(np.exp2(scales.astype(np.float64) - 127.0), 8, axis=1)[..., None]
    return vals.transpose(0, 1, 3, 2).reshape(g * 512, n)


def gelu(v):
    return 0.5 * v * (1.0 + np.tanh(np.sqrt(2.0 / np.pi) * (v + 0.044715 * v**3)))


K, H, N, T, S = 1536, 512, 768, 2048, 1024

def setup_inputs():
    n = np.random.standard_normal
    s = mx_kscale(K)[:, None]
    u = mx_kscale(H)[:, None]
    tab_words, tab_scales = pack_weight(n((K, T)) * s, "e4m3")
    w4_words, w4_scales = pack_weight(n((H, N)) / np.sqrt(H) / u, "e2m1")
    return {
        "tab_words": tab_words, "tab_scales": tab_scales,
        "offs": striped(np.random.permutation(T)[:S]),
        "w1": (0.7 * n((K, H)) / np.sqrt(K) / s).astype(np.float32),
        "gT": (0.7 * n((H, T))).astype(np.float32),
        "gain": (np.exp(0.3 * n(H)) * u[:, 0]).astype(np.float32),
        "w4_words": w4_words, "w4_scales": w4_scales,
    }

def reference(tab_words, tab_scales, offs, w1, gT, gain, w4_words, w4_scales):
    idx = unstriped(offs)
    v = unpack_weight(tab_words, tab_scales, "e4m3")[:, unstriped(offs)]
    g = f64(gT)[:, idx]
    w1q = mxq(f64(w1), 0, "e4m3")
    a = w1q.T @ v
    d = a - g
    h = f64(gain)[:, None] * np.exp(-np.square(d))
    hq = mxq(h, 0, "e4m3")
    w4 = unpack_weight(w4_words, w4_scales, "e2m1")
    return w4.T @ hq

@@ -1,0 +1,191 @@
+from contextlib import ExitStack
+
+import concourse.mybir as mybir
+
+K, H, N, T, S = 1536, 512, 768, 2048, 1024
+FLOPS = 2 * K * H * S + 2 * H * N * S
+
+F32 = mybir.dt.float32
+BF16 = mybir.dt.bfloat16
+I32 = mybir.dt.int32
+U32 = mybir.dt.uint32
+U16 = mybir.dt.uint16
+U8 = mybir.dt.uint8
+FP8X4 = mybir.dt.float8_e4m3fn_x4
+FP4X4 = mybir.dt.float4_e2m1fn_x4
+ACT = mybir.ActivationFunctionType
+ALU = mybir.AluOpType
+
+P = 128
+PACK = 4
+PASSES = K // (P * PACK)
+BANK = 512
+CHUNK = 256
+CHUNKS = S // CHUNK
+N_TILES = N // P
+
+
+def tile_list_ball_gauss_features_kernel(tc, tab_words, tab_scales, offs, w1, gT, gain, w4_words, w4_scales, out):
+    nc = tc.nc
+    with ExitStack() as ctx:
+        held = ctx.enter_context(tc.tile_pool(name="held", bufs=1))
+        ring = ctx.enter_context(tc.tile_pool(name="ring", bufs=4))
+        psum_a = ctx.enter_context(tc.psum_pool(name="psum_a", bufs=4))
+        psum_o = ctx.enter_context(tc.psum_pool(name="psum_o", bufs=4))
+
+        offsets = held.tile([P, S // 16], U16, name="offsets")
+        nc.sync.dma_start(offsets[:], offs)
+
+        def listed(window, j0, j1):
+            return window.indirect(offsets[:, j0 // 16 : j1 // 16])
+
+        tab_planes = held.tile([P, T // 4], I32, name="tab_planes", align_bytes=64)
+        w4_plane = held.tile([P, N // 4], I32, name="w4_plane", align_bytes=64)
+        nc.vector.memset(tab_planes[:], 0)
+        nc.vector.memset(w4_plane[:], 0)
+        warm = held.tile([P, 8], F32, name="warm")
+        warm_out = held.tile([P, 8], F32, name="warm_out")
+        nc.vector.memset(warm[:], 0.0)
+        nc.scalar.activation(warm_out[:], warm[:], ACT.Exp)
+
+        tab_scale_words = tab_scales.bitcast(I32)
+        for q in range(4):
+            nc.scalar.dma_start(out=tab_planes[32 * q : 32 * q + 4 * PASSES, :], in_=tab_scale_words[:, 4 * q : 4 * q + 4, :])
+        gains = held.tile([P, PACK], F32, name="gains")
+        nc.scalar.dma_start(out=gains[:], in_=gain.rearrange("(p t) -> p t", t=PACK))
+
+        tab = []
+        for a in range(PASSES):
+            words = held.tile([P, T], I32, name="tab%d" % a, align_bytes=64)
+            nc.sync.dma_start(out=words[:], in_=tab_words[a].rearrange("p n t -> p (n t)").bitcast(I32))
+            tab.append(words)
+        w_raw = []
+        for a in range(PASSES):
+            raw = held.tile([P, PACK, H], F32, name="w_raw%d" % a)
+            nc.sync.dma_start(out=raw[:], in_=w1[a * 512 : (a + 1) * 512, :].rearrange("(p j) c -> p j c", j=PACK))
+            w_raw.append(raw)
+        centers = []
+        g_rows = gT.rearrange("(p t) c -> t p c", t=PACK)
+        for t in range(PACK):
+            rows = held.tile([P, T], F32, name="centers%d" % t)
+            nc.sync.dma_start(out=rows[:], in_=g_rows[t])
+            centers.append(rows)
+        w4 = held.tile([P, 2 * N], U8, name="w4", align_bytes=64)
+        nc.sync.dma_start(out=w4[:], in_=w4_words[0])
+        w4_scale_words = w4_scales[0].bitcast(I32)
+        for q in range(4):
+            nc.sync.dma_start(out=w4_plane[32 * q : 32 * q + 4, :], in_=w4_scale_words[4 * q : 4 * q + 4, :])
+
+        v_words = [held.tile([P, S], U32, name="v_words%d" % a, align_bytes=64) for a in range(PASSES)]
+        v_planes = held.tile([P, S], U8, name="v_planes", align_bytes=64)
+        nc.vector.tensor_copy(v_words[0][:], listed(tab[0][:].bitcast(U32), 0, S))
+        nc.vector.tensor_copy(v_planes[:], listed(tab_planes[:].bitcast(U8), 0, S))
+        for a in range(1, PASSES):
+            nc.vector.tensor_copy(v_words[a][:], listed(tab[a][:].bitcast(U32), 0, S))
+
+        w_codes, w_planes = [], []
+        for a in range(PASSES):
+            grouped = held.tile([P, PACK * H], BF16, name="w_grouped%d" % a, align_bytes=64)
+            src = w_raw[a][:].rearrange("p j (m t) -> p m j t", t=PACK)
+            dst = grouped[:].rearrange("p (t m j) -> p m j t", t=PACK, j=PACK)
+            if a < PASSES - 1:
+                nc.scalar.copy(dst, src)
+            else:
+                nc.vector.tensor_copy(dst, src)
+            codes = held.tile([P, H], U32, name="w_codes%d" % a, align_bytes=64)
+            plane = held.tile([P, H], U8, name="w_plane%d" % a, align_bytes=64)
+            nc.vector.quantize_mx(out=codes[:].bitcast(FP8X4), scales=plane[:], in_=grouped[:])
+            w_codes.append(codes)
+            w_planes.append(plane)
+
+        e = held.tile([P, CHUNKS, PACK, CHUNK], F32, name="e")
+
+        def project(acc, t, j0, j1):
+            for a in range(PASSES):
+                nc.tensor.matmul_mx(
+                    out=acc,
+                    lhsT=w_codes[a][:, t * P : (t + 1) * P].bitcast(FP8X4),
+                    lhsT_scale=w_planes[a][:, t * P : (t + 1) * P],
+                    rhs=v_words[a][:, j0:j1].bitcast(FP8X4),
+                    rhs_scale=v_planes[4 * a : P, j0:j1],
+                    start=(a == 0),
+                    stop=(a == PASSES - 1),
+                )
+
+        for t in range(2):
+            for j0 in range(0, S, BANK):
+                j1 = j0 + BANK
+                acc = psum_a.tile([P, BANK], F32, name="acc")
+                project(acc[:], t, j0, j1)
+                picked = ring.tile([P, BANK], F32, name="picked")
+                d = ring.tile([P, BANK], F32, name="d")
+                nc.vector.tensor_copy(picked[:], listed(centers[t][:], j0, j1))
+                nc.vector.tensor_tensor(d[:], acc[:], picked[:], ALU.subtract)
+                nc.scalar.activation(d[:], d[:], ACT.Square)
+                nc.scalar.activation(
+                    e[:, j0 // CHUNK : j1 // CHUNK, t, :], d[:].rearrange("p (c j) -> p c j", j=CHUNK), ACT.Exp, scale=-1.0
+                )
+
+        out_rows = out.rearrange("(n p) j -> p n j", p=P)
+
+        def respond(j0, j1):
+            acc = psum_a.tile([P, 2, CHUNK], F32, name="acc")
+            picked = ring.tile([P, 2, CHUNK], F32, name="picked")
+            d = ring.tile([P, 2, CHUNK], F32, name="d")
+            for t in (2, 3):
+                project(acc[:, t - 2, :], t, j0, j1)
+                nc.vector.tensor_copy(picked[:, t - 2, :], listed(centers[t][:], j0, j1))
+            nc.vector.tensor_tensor(d[:], acc[:], picked[:], ALU.subtract)
+            nc.scalar.activation(d[:], d[:], ACT.Square)
+            nc.scalar.activation(e[:, j0 // CHUNK, 2:4, :], d[:], ACT.Exp, scale=-1.0)
+
+        def weigh(j0, j1):
+            width = j1 - j0
+            h = ring.tile([P, PACK * width], BF16, name="h", align_bytes=64)
+            nc.vector.tensor_tensor(
+                h[:].rearrange("p (c i t) -> p c t i", i=4, t=PACK),
+                e[:, j0 // CHUNK, :, j0 % CHUNK : j0 % CHUNK + width].rearrange("p t (c i) -> p c t i", i=4),
+                gains[:].rearrange("p (c t i) -> p c t i", c=1, i=1).to_broadcast([P, width // 4, PACK, 4]),
+                ALU.mult,
+            )
+            return h
+
+        def mix(h, j0, j1, flip):
+            width = j1 - j0
+            h_codes = ring.tile([P, width], U32, name="h_codes", align_bytes=64)
+            h_plane = ring.tile([P, width], U8, name="h_plane", align_bytes=64)
+            nc.vector.quantize_mx(out=h_codes[:].bitcast(FP8X4), scales=h_plane[:], in_=h[:])
+            per_bank = BANK // width
+            for b, n0 in enumerate(range(0, N_TILES, per_bank)):
+                count = min(per_bank, N_TILES - n0)
+                acc = psum_o.tile([P, count, width], F32, name="features")
+                for i in range(count):
+                    n = n0 + i
+                    nc.tensor.matmul_mx(
+                        out=acc[:, i, :],
+                        lhsT=w4[:, 2 * P * n : 2 * P * (n + 1)].bitcast(FP4X4),
+                        lhsT_scale=w4_plane[:].bitcast(U8)[:, P * n : P * (n + 1)],
+                        rhs=h_codes[:].bitcast(FP8X4),
+                        rhs_scale=h_plane[:],
+                        start=True,
+                        stop=True,
+                    )
+                staged = ring.tile([P, count, width], F32, name="staged", bufs=8)
+                if flip and b == 1:
+                    nc.vector.tensor_copy(staged[:], acc[:])
+                else:
+                    nc.scalar.copy(staged[:], acc[:])
+                nc.sync.dma_start(out=out_rows[:, n0 : n0 + count, j0:j1], in_=staged[:])
+
+        respond(0, CHUNK)
+        for c in range(CHUNKS - 1):
+            j0 = c * CHUNK
+            h = weigh(j0, j0 + CHUNK)
+            respond(j0 + CHUNK, j0 + 2 * CHUNK)
+            mix(h, j0, j0 + CHUNK, False)
+        j0 = S - CHUNK
+        half = CHUNK // 2
+        h0 = weigh(j0, j0 + half)
+        h1 = weigh(j0 + half, S)
+        mix(h0, j0, j0 + half, False)
+        mix(h1, j0 + half, S, True)

@@ -19,17 +19,28 @@ ALU = mybir.AluOpType
 P = 128
 PACK = 4
 PASSES = K // (P * PACK)
+QUADRANTS = 4
+SCALE_ROWS = 4
 BANK = 512
 CHUNK = 256
 CHUNKS = S // CHUNK
 N_TILES = N // P
+RUN = 4
+
+HALVES = [(t, j0) for t in (0, 1) for j0 in range(0, S, BANK)]
+LATE_SLOTS = (2, 3)
+
+SCALAR_ALONE = [(0, P, False)]
+LAST_PASS_SHARES = [(0, P // 2, False), (P // 2, 3 * P // 4, False), (3 * P // 4, P, True)]
+
+BANKS_ON_VECTOR = [(), (2,), (), (0, 2)]
 
 
 def tile_list_ball_gauss_features_kernel(tc, tab_words, tab_scales, offs, w1, gT, gain, w4_words, w4_scales, out):
     nc = tc.nc
     with ExitStack() as ctx:
         held = ctx.enter_context(tc.tile_pool(name="held", bufs=1))
-        ring = ctx.enter_context(tc.tile_pool(name="ring", bufs=4))
+        ring = ctx.enter_context(tc.tile_pool(name="ring", bufs=CHUNKS))
         psum_a = ctx.enter_context(tc.psum_pool(name="psum_a", bufs=4))
         psum_o = ctx.enter_context(tc.psum_pool(name="psum_o", bufs=4))
 
@@ -39,128 +50,141 @@ def tile_list_ball_gauss_features_kernel(tc, tab_words, tab_scales, offs, w1, gT
         def listed(window, j0, j1):
             return window.indirect(offsets[:, j0 // 16 : j1 // 16])
 
-        tab_planes = held.tile([P, T // 4], I32, name="tab_planes", align_bytes=64)
+        tab_planes = held.tile([P, T // 4], I32, name="tab_planes", tag="planes_then_codes", align_bytes=64)
         w4_plane = held.tile([P, N // 4], I32, name="w4_plane", align_bytes=64)
         nc.vector.memset(tab_planes[:], 0)
         nc.vector.memset(w4_plane[:], 0)
-        warm = held.tile([P, 8], F32, name="warm")
-        warm_out = held.tile([P, 8], F32, name="warm_out")
-        nc.vector.memset(warm[:], 0.0)
-        nc.scalar.activation(warm_out[:], warm[:], ACT.Exp)
-
         tab_scale_words = tab_scales.bitcast(I32)
-        for q in range(4):
-            nc.scalar.dma_start(out=tab_planes[32 * q : 32 * q + 4 * PASSES, :], in_=tab_scale_words[:, 4 * q : 4 * q + 4, :])
+        for q in range(QUADRANTS):
+            nc.sync.dma_start(
+                out=tab_planes[32 * q : 32 * q + SCALE_ROWS * PASSES, :],
+                in_=tab_scale_words[:, SCALE_ROWS * q : SCALE_ROWS * (q + 1), :],
+            )
         gains = held.tile([P, PACK], F32, name="gains")
         nc.scalar.dma_start(out=gains[:], in_=gain.rearrange("(p t) -> p t", t=PACK))
+        warm = held.tile([P, PACK], F32, name="warm")
+        nc.scalar.activation(warm[:], gains[:], ACT.Exp, scale=0.0)
 
         tab = []
         for a in range(PASSES):
             words = held.tile([P, T], I32, name="tab%d" % a, align_bytes=64)
-            nc.sync.dma_start(out=words[:], in_=tab_words[a].rearrange("p n t -> p (n t)").bitcast(I32))
+            nc.sync.dma_start(out=words[:], in_=tab_words[a].rearrange("p n i -> p (n i)").bitcast(I32))
             tab.append(words)
-        w_raw = []
-        for a in range(PASSES):
-            raw = held.tile([P, PACK, H], F32, name="w_raw%d" % a)
-            nc.sync.dma_start(out=raw[:], in_=w1[a * 512 : (a + 1) * 512, :].rearrange("(p j) c -> p j c", j=PACK))
-            w_raw.append(raw)
-        centers = []
-        g_rows = gT.rearrange("(p t) c -> t p c", t=PACK)
-        for t in range(PACK):
-            rows = held.tile([P, T], F32, name="centers%d" % t)
-            nc.sync.dma_start(out=rows[:], in_=g_rows[t])
-            centers.append(rows)
+
+        w_raw = held.tile([P, PASSES * PACK, H], F32, name="w_raw")
+        centers = [held.tile([P, T], F32, name="centers%d" % t) for t in range(PACK)]
+        center_rows = gT.rearrange("(p t) c -> t p c", t=PACK)
+
+        def load_w(a, c0, c1):
+            rows = w1[a * P * PACK : (a + 1) * P * PACK, :].rearrange("(p i) c -> p i c", i=PACK)
+            nc.sync.dma_start(out=w_raw[:, a * PACK : (a + 1) * PACK, c0:c1], in_=rows[:, :, c0:c1])
+
+        load_w(0, 0, H)
+        load_w(1, 0, H)
+        for t in (0, 1):
+            nc.sync.dma_start(out=centers[t][:], in_=center_rows[t])
+        load_w(2, 0, H // 2)
+        load_w(2, H // 2, H)
+        for t in LATE_SLOTS:
+            nc.sync.dma_start(out=centers[t][:], in_=center_rows[t])
         w4 = held.tile([P, 2 * N], U8, name="w4", align_bytes=64)
         nc.sync.dma_start(out=w4[:], in_=w4_words[0])
         w4_scale_words = w4_scales[0].bitcast(I32)
-        for q in range(4):
-            nc.sync.dma_start(out=w4_plane[32 * q : 32 * q + 4, :], in_=w4_scale_words[4 * q : 4 * q + 4, :])
+        for q in range(QUADRANTS):
+            nc.sync.dma_start(
+                out=w4_plane[32 * q : 32 * q + SCALE_ROWS, :],
+                in_=w4_scale_words[SCALE_ROWS * q : SCALE_ROWS * (q + 1), :],
+            )
 
         v_words = [held.tile([P, S], U32, name="v_words%d" % a, align_bytes=64) for a in range(PASSES)]
         v_planes = held.tile([P, S], U8, name="v_planes", align_bytes=64)
-        nc.vector.tensor_copy(v_words[0][:], listed(tab[0][:].bitcast(U32), 0, S))
-        nc.vector.tensor_copy(v_planes[:], listed(tab_planes[:].bitcast(U8), 0, S))
-        for a in range(1, PASSES):
-            nc.vector.tensor_copy(v_words[a][:], listed(tab[a][:].bitcast(U32), 0, S))
-
-        w_codes, w_planes = [], []
         for a in range(PASSES):
-            grouped = held.tile([P, PACK * H], BF16, name="w_grouped%d" % a, align_bytes=64)
-            src = w_raw[a][:].rearrange("p j (m t) -> p m j t", t=PACK)
-            dst = grouped[:].rearrange("p (t m j) -> p m j t", t=PACK, j=PACK)
-            if a < PASSES - 1:
-                nc.scalar.copy(dst, src)
-            else:
-                nc.vector.tensor_copy(dst, src)
-            codes = held.tile([P, H], U32, name="w_codes%d" % a, align_bytes=64)
-            plane = held.tile([P, H], U8, name="w_plane%d" % a, align_bytes=64)
-            nc.vector.quantize_mx(out=codes[:].bitcast(FP8X4), scales=plane[:], in_=grouped[:])
-            w_codes.append(codes)
-            w_planes.append(plane)
+            nc.vector.tensor_copy(v_words[a][:], listed(tab[a][:].bitcast(U32), 0, S))
+        nc.vector.tensor_copy(v_planes[:], listed(tab_planes[:].bitcast(U8), 0, S))
 
-        e = held.tile([P, CHUNKS, PACK, CHUNK], F32, name="e")
+        w_grouped = [held.tile([P, PACK * H], BF16, name="w_grouped%d" % i, align_bytes=64) for i in range(2)]
+        w_codes = [
+            held.tile([P, H], U32, name="w_codes%d" % a, tag="planes_then_codes" if a == 0 else "w_codes%d" % a, align_bytes=64)
+            for a in range(PASSES)
+        ]
+        w_planes = [held.tile([P, H], U8, name="w_plane%d" % a, align_bytes=64) for a in range(PASSES)]
 
-        def project(acc, t, j0, j1):
-            for a in range(PASSES):
-                nc.tensor.matmul_mx(
-                    out=acc,
-                    lhsT=w_codes[a][:, t * P : (t + 1) * P].bitcast(FP8X4),
-                    lhsT_scale=w_planes[a][:, t * P : (t + 1) * P],
-                    rhs=v_words[a][:, j0:j1].bitcast(FP8X4),
-                    rhs_scale=v_planes[4 * a : P, j0:j1],
-                    start=(a == 0),
-                    stop=(a == PASSES - 1),
-                )
+        def quantize_w(a, shares):
+            grouped = w_grouped[a % 2]
+            src = w_raw[:, a * PACK : (a + 1) * PACK, :].rearrange("p i (m t) -> p m i t", t=PACK)
+            dst = grouped[:].rearrange("p (t m i) -> p m i t", t=PACK, i=PACK)
+            for m0, m1, on_vector in shares:
+                if on_vector:
+                    nc.vector.tensor_copy(dst[:, m0:m1], src[:, m0:m1])
+                else:
+                    nc.scalar.copy(dst[:, m0:m1], src[:, m0:m1])
+            nc.vector.quantize_mx(out=w_codes[a][:].bitcast(FP8X4), scales=w_planes[a][:], in_=grouped[:])
 
-        for t in range(2):
-            for j0 in range(0, S, BANK):
-                j1 = j0 + BANK
-                acc = psum_a.tile([P, BANK], F32, name="acc")
-                project(acc[:], t, j0, j1)
-                picked = ring.tile([P, BANK], F32, name="picked")
-                d = ring.tile([P, BANK], F32, name="d")
-                nc.vector.tensor_copy(picked[:], listed(centers[t][:], j0, j1))
-                nc.vector.tensor_tensor(d[:], acc[:], picked[:], ALU.subtract)
-                nc.scalar.activation(d[:], d[:], ACT.Square)
-                nc.scalar.activation(
-                    e[:, j0 // CHUNK : j1 // CHUNK, t, :], d[:].rearrange("p (c j) -> p c j", j=CHUNK), ACT.Exp, scale=-1.0
-                )
+        work = held.tile([P, CHUNKS, 2 + PACK, CHUNK], F32, name="work")
+        d_half = held.tile([P, len(HALVES), BANK], F32, name="d_half")
+        h = held.tile([P, CHUNKS, CHUNK * PACK], BF16, name="h", align_bytes=64)
 
+        pieces = w_raw[:].rearrange("p r (b j) -> p (r b) j", j=CHUNK)
+        chunk_centers = [pieces[:, 16:18, :], pieces[:, 18:20, :], pieces[:, 0:5:4, :], pieces[:, 2:7:4, :]]
         out_rows = out.rearrange("(n p) j -> p n j", p=P)
 
-        def respond(j0, j1):
-            acc = psum_a.tile([P, 2, CHUNK], F32, name="acc")
-            picked = ring.tile([P, 2, CHUNK], F32, name="picked")
-            d = ring.tile([P, 2, CHUNK], F32, name="d")
-            for t in (2, 3):
-                project(acc[:, t - 2, :], t, j0, j1)
-                nc.vector.tensor_copy(picked[:, t - 2, :], listed(centers[t][:], j0, j1))
-            nc.vector.tensor_tensor(d[:], acc[:], picked[:], ALU.subtract)
-            nc.scalar.activation(d[:], d[:], ACT.Square)
-            nc.scalar.activation(e[:, j0 // CHUNK, 2:4, :], d[:], ACT.Exp, scale=-1.0)
+        def project(acc, t, j0, j1, a):
+            nc.tensor.matmul_mx(
+                out=acc,
+                lhsT=w_codes[a][:, t * P : (t + 1) * P].bitcast(FP8X4),
+                lhsT_scale=w_planes[a][:, t * P : (t + 1) * P],
+                rhs=v_words[a][:, j0:j1].bitcast(FP8X4),
+                rhs_scale=v_planes[SCALE_ROWS * a : P, j0:j1],
+                start=(a == 0),
+                stop=(a == PASSES - 1),
+            )
 
-        def weigh(j0, j1):
-            width = j1 - j0
-            h = ring.tile([P, PACK * width], BF16, name="h", align_bytes=64)
+        def half_gather(u):
+            t, j0 = HALVES[u]
+            nc.vector.tensor_copy(w_raw[:, u, :], listed(centers[t][:], j0, j0 + BANK))
+
+        def half_gauss(u):
+            t, j0 = HALVES[u]
+            d = d_half[:, u, :]
+            c = j0 // CHUNK
+            nc.vector.tensor_tensor(d, half_acc[u][:], w_raw[:, u, :], ALU.subtract)
+            nc.scalar.activation(d, d, ACT.Square)
+            nc.scalar.activation(work[:, c : c + 2, 2 + t, :], d.rearrange("p (c j) -> p c j", j=CHUNK), ACT.Exp, scale=-1.0)
+
+        chunk_acc = {}
+
+        def chunk_project(c):
+            acc = psum_a.tile([P, 2, CHUNK], F32, name="acc")
+            for t in LATE_SLOTS:
+                for a in range(PASSES):
+                    project(acc[:, t - 2, :], t, c * CHUNK, (c + 1) * CHUNK, a)
+            chunk_acc[c] = acc
+
+        def chunk_gather(c, t):
+            nc.vector.tensor_copy(chunk_centers[c][:, t - 2, :], listed(centers[t][:], c * CHUNK, (c + 1) * CHUNK))
+
+        def chunk_gauss(c):
+            d = work[:, c, 0:2, :]
+            nc.vector.tensor_tensor(d, chunk_acc[c][:], chunk_centers[c], ALU.subtract)
+            nc.scalar.activation(d, d, ACT.Square)
+            nc.scalar.activation(work[:, c, 4:6, :], d, ACT.Exp, scale=-1.0)
+
+        def weigh(c):
             nc.vector.tensor_tensor(
-                h[:].rearrange("p (c i t) -> p c t i", i=4, t=PACK),
-                e[:, j0 // CHUNK, :, j0 % CHUNK : j0 % CHUNK + width].rearrange("p t (c i) -> p c t i", i=4),
-                gains[:].rearrange("p (c t i) -> p c t i", c=1, i=1).to_broadcast([P, width // 4, PACK, 4]),
+                h[:, c, :].rearrange("p (g i t) -> p g t i", i=RUN, t=PACK),
+                work[:, c, 2:, :].rearrange("p t (g i) -> p g t i", i=RUN),
+                gains[:].rearrange("p (g t i) -> p g t i", g=1, i=1).to_broadcast([P, CHUNK // RUN, PACK, RUN]),
                 ALU.mult,
             )
-            return h
 
-        def mix(h, j0, j1, flip):
-            width = j1 - j0
-            h_codes = ring.tile([P, width], U32, name="h_codes", align_bytes=64)
-            h_plane = ring.tile([P, width], U8, name="h_plane", align_bytes=64)
-            nc.vector.quantize_mx(out=h_codes[:].bitcast(FP8X4), scales=h_plane[:], in_=h[:])
-            per_bank = BANK // width
-            for b, n0 in enumerate(range(0, N_TILES, per_bank)):
-                count = min(per_bank, N_TILES - n0)
-                acc = psum_o.tile([P, count, width], F32, name="features")
-                for i in range(count):
-                    n = n0 + i
+        def mix(c):
+            h_codes = ring.tile([P, CHUNK], U32, name="h_codes", align_bytes=64)
+            h_plane = ring.tile([P, CHUNK], U8, name="h_plane", align_bytes=64)
+            nc.vector.quantize_mx(out=h_codes[:].bitcast(FP8X4), scales=h_plane[:], in_=h[:, c, :])
+            for b in range(N_TILES // 2):
+                acc = psum_o.tile([P, 2, CHUNK], F32, name="features")
+                for i in range(2):
+                    n = 2 * b + i
                     nc.tensor.matmul_mx(
                         out=acc[:, i, :],
                         lhsT=w4[:, 2 * P * n : 2 * P * (n + 1)].bitcast(FP4X4),
@@ -170,22 +194,48 @@ def tile_list_ball_gauss_features_kernel(tc, tab_words, tab_scales, offs, w1, gT
                         start=True,
                         stop=True,
                     )
-                staged = ring.tile([P, count, width], F32, name="staged", bufs=8)
-                if flip and b == 1:
+                staged = ring.tile([P, 2, CHUNK], F32, name="staged", bufs=CHUNKS * N_TILES // 2)
+                if b in BANKS_ON_VECTOR[c]:
                     nc.vector.tensor_copy(staged[:], acc[:])
                 else:
                     nc.scalar.copy(staged[:], acc[:])
-                nc.sync.dma_start(out=out_rows[:, n0 : n0 + count, j0:j1], in_=staged[:])
+                nc.sync.dma_start(out=out_rows[:, 2 * b : 2 * b + 2, c * CHUNK : (c + 1) * CHUNK], in_=staged[:])
 
-        respond(0, CHUNK)
-        for c in range(CHUNKS - 1):
-            j0 = c * CHUNK
-            h = weigh(j0, j0 + CHUNK)
-            respond(j0 + CHUNK, j0 + 2 * CHUNK)
-            mix(h, j0, j0 + CHUNK, False)
-        j0 = S - CHUNK
-        half = CHUNK // 2
-        h0 = weigh(j0, j0 + half)
-        h1 = weigh(j0 + half, S)
-        mix(h0, j0, j0 + half, False)
-        mix(h1, j0 + half, S, True)
+        quantize_w(0, SCALAR_ALONE)
+        quantize_w(1, SCALAR_ALONE)
+        for u in range(len(HALVES)):
+            half_gather(u)
+        quantize_w(2, LAST_PASS_SHARES)
+        half_acc = [psum_a.tile([P, BANK], F32, name="acc") for u in range(len(HALVES))]
+        for a in range(PASSES):
+            for u in (0, 2, 1, 3):
+                t, j0 = HALVES[u]
+                project(half_acc[u][:], t, j0, j0 + BANK, a)
+
+        chunk_gather(0, 2)
+        chunk_gather(1, 2)
+        half_gauss(0)
+        chunk_project(0)
+        half_gauss(2)
+        chunk_project(1)
+        chunk_gather(0, 3)
+        chunk_gather(1, 3)
+        chunk_gauss(0)
+        half_gauss(1)
+        chunk_project(2)
+        chunk_gather(2, 2)
+        chunk_gather(2, 3)
+        chunk_gauss(1)
+        chunk_project(3)
+        half_gauss(3)
+        weigh(0)
+        chunk_gauss(2)
+        mix(0)
+        weigh(1)
+        chunk_gather(3, 3)
+        chunk_gather(3, 2)
+        mix(1)
+        chunk_gauss(3)
+        for c in (2, 3):
+            weigh(c)
+            mix(c)

@@ -33,14 +33,14 @@ LATE_SLOTS = (2, 3)
 SCALAR_ALONE = [(0, P, False)]
 LAST_PASS_SHARES = [(0, P // 2, False), (P // 2, 3 * P // 4, False), (3 * P // 4, P, True)]
 
-BANKS_ON_VECTOR = [(), (2,), (), (0, 2)]
+TILES_ON_VECTOR = [(), (0, 2, 4)]
 
 
 def tile_list_ball_gauss_features_kernel(tc, tab_words, tab_scales, offs, w1, gT, gain, w4_words, w4_scales, out):
     nc = tc.nc
     with ExitStack() as ctx:
         held = ctx.enter_context(tc.tile_pool(name="held", bufs=1))
-        ring = ctx.enter_context(tc.tile_pool(name="ring", bufs=CHUNKS))
+        ring = ctx.enter_context(tc.tile_pool(name="ring", bufs=S // BANK))
         psum_a = ctx.enter_context(tc.psum_pool(name="psum_a", bufs=4))
         psum_o = ctx.enter_context(tc.psum_pool(name="psum_o", bufs=4))
 
@@ -62,8 +62,6 @@ def tile_list_ball_gauss_features_kernel(tc, tab_words, tab_scales, offs, w1, gT
             )
         gains = held.tile([P, PACK], F32, name="gains")
         nc.scalar.dma_start(out=gains[:], in_=gain.rearrange("(p t) -> p t", t=PACK))
-        warm = held.tile([P, PACK], F32, name="warm")
-        nc.scalar.activation(warm[:], gains[:], ACT.Exp, scale=0.0)
 
         tab = []
         for a in range(PASSES):
@@ -122,11 +120,10 @@ def tile_list_ball_gauss_features_kernel(tc, tab_words, tab_scales, offs, w1, gT
 
         work = held.tile([P, CHUNKS, 2 + PACK, CHUNK], F32, name="work")
         d_half = held.tile([P, len(HALVES), BANK], F32, name="d_half")
-        h = held.tile([P, CHUNKS, CHUNK * PACK], BF16, name="h", align_bytes=64)
+        h = held.tile([P, 2, CHUNK * PACK], BF16, name="h", align_bytes=64)
 
         pieces = w_raw[:].rearrange("p r (b j) -> p (r b) j", j=CHUNK)
         chunk_centers = [pieces[:, 16:18, :], pieces[:, 18:20, :], pieces[:, 0:5:4, :], pieces[:, 2:7:4, :]]
-        out_rows = out.rearrange("(n p) j -> p n j", p=P)
 
         def project(acc, t, j0, j1, a):
             nc.tensor.matmul_mx(
@@ -171,35 +168,33 @@ def tile_list_ball_gauss_features_kernel(tc, tab_words, tab_scales, offs, w1, gT
 
         def weigh(c):
             nc.vector.tensor_tensor(
-                h[:, c, :].rearrange("p (g i t) -> p g t i", i=RUN, t=PACK),
+                h[:, c % 2, :].rearrange("p (g i t) -> p g t i", i=RUN, t=PACK),
                 work[:, c, 2:, :].rearrange("p t (g i) -> p g t i", i=RUN),
                 gains[:].rearrange("p (g t i) -> p g t i", g=1, i=1).to_broadcast([P, CHUNK // RUN, PACK, RUN]),
                 ALU.mult,
             )
 
-        def mix(c):
-            h_codes = ring.tile([P, CHUNK], U32, name="h_codes", align_bytes=64)
-            h_plane = ring.tile([P, CHUNK], U8, name="h_plane", align_bytes=64)
-            nc.vector.quantize_mx(out=h_codes[:].bitcast(FP8X4), scales=h_plane[:], in_=h[:, c, :])
-            for b in range(N_TILES // 2):
-                acc = psum_o.tile([P, 2, CHUNK], F32, name="features")
-                for i in range(2):
-                    n = 2 * b + i
-                    nc.tensor.matmul_mx(
-                        out=acc[:, i, :],
-                        lhsT=w4[:, 2 * P * n : 2 * P * (n + 1)].bitcast(FP4X4),
-                        lhsT_scale=w4_plane[:].bitcast(U8)[:, P * n : P * (n + 1)],
-                        rhs=h_codes[:].bitcast(FP8X4),
-                        rhs_scale=h_plane[:],
-                        start=True,
-                        stop=True,
-                    )
-                staged = ring.tile([P, 2, CHUNK], F32, name="staged", bufs=CHUNKS * N_TILES // 2)
-                if b in BANKS_ON_VECTOR[c]:
+        def mix(half):
+            h_codes = ring.tile([P, BANK], U32, name="h_codes", align_bytes=64)
+            h_plane = ring.tile([P, BANK], U8, name="h_plane", align_bytes=64)
+            nc.vector.quantize_mx(out=h_codes[:].bitcast(FP8X4), scales=h_plane[:], in_=h[:].rearrange("p c w -> p (c w)"))
+            for n in range(N_TILES):
+                acc = psum_o.tile([P, BANK], F32, name="features")
+                nc.tensor.matmul_mx(
+                    out=acc[:],
+                    lhsT=w4[:, 2 * P * n : 2 * P * (n + 1)].bitcast(FP4X4),
+                    lhsT_scale=w4_plane[:].bitcast(U8)[:, P * n : P * (n + 1)],
+                    rhs=h_codes[:].bitcast(FP8X4),
+                    rhs_scale=h_plane[:],
+                    start=True,
+                    stop=True,
+                )
+                staged = ring.tile([P, BANK], F32, name="staged", bufs=N_TILES * S // BANK)
+                if n in TILES_ON_VECTOR[half]:
                     nc.vector.tensor_copy(staged[:], acc[:])
                 else:
                     nc.scalar.copy(staged[:], acc[:])
-                nc.sync.dma_start(out=out_rows[:, 2 * b : 2 * b + 2, c * CHUNK : (c + 1) * CHUNK], in_=staged[:])
+                nc.sync.dma_start(out=out[P * n : P * (n + 1), half * BANK : (half + 1) * BANK], in_=staged[:])
 
         quantize_w(0, SCALAR_ALONE)
         quantize_w(1, SCALAR_ALONE)
@@ -229,13 +224,12 @@ def tile_list_ball_gauss_features_kernel(tc, tab_words, tab_scales, offs, w1, gT
         chunk_project(3)
         half_gauss(3)
         weigh(0)
+        weigh(1)
         chunk_gauss(2)
         mix(0)
-        weigh(1)
         chunk_gather(3, 3)
         chunk_gather(3, 2)
-        mix(1)
         chunk_gauss(3)
-        for c in (2, 3):
-            weigh(c)
-            mix(c)
+        weigh(2)
+        weigh(3)
+        mix(1)

@@ -25,24 +25,16 @@ BANK = 512
 CHUNK = 256
 CHUNKS = S // CHUNK
 N_TILES = N // P
-RUN = 4
-
-HALVES = [(t, j0) for t in (0, 1) for j0 in range(0, S, BANK)]
-LATE_SLOTS = (2, 3)
-
-SCALAR_ALONE = [(0, P, False)]
-LAST_PASS_SHARES = [(0, P // 2, False), (P // 2, 3 * P // 4, False), (3 * P // 4, P, True)]
-
-TILES_ON_VECTOR = [(), (0, 2, 4)]
+RUN = 2
+PROJECT_ORDER = [(t, u) for t in range(PACK) for u in range(2)]
+W2_ON_SCALAR = 48
 
 
 def tile_list_ball_gauss_features_kernel(tc, tab_words, tab_scales, offs, w1, gT, gain, w4_words, w4_scales, out):
     nc = tc.nc
     with ExitStack() as ctx:
         held = ctx.enter_context(tc.tile_pool(name="held", bufs=1))
-        ring = ctx.enter_context(tc.tile_pool(name="ring", bufs=S // BANK))
-        psum_a = ctx.enter_context(tc.psum_pool(name="psum_a", bufs=4))
-        psum_o = ctx.enter_context(tc.psum_pool(name="psum_o", bufs=4))
+        psum = ctx.enter_context(tc.psum_pool(name="psum", bufs=8))
 
         offsets = held.tile([P, S // 16], U16, name="offsets")
         nc.sync.dma_start(offsets[:], offs)
@@ -50,186 +42,203 @@ def tile_list_ball_gauss_features_kernel(tc, tab_words, tab_scales, offs, w1, gT
         def listed(window, j0, j1):
             return window.indirect(offsets[:, j0 // 16 : j1 // 16])
 
-        tab_planes = held.tile([P, T // 4], I32, name="tab_planes", tag="planes_then_codes", align_bytes=64)
-        w4_plane = held.tile([P, N // 4], I32, name="w4_plane", align_bytes=64)
+        tab_planes = held.tile([P, T // 4], I32, name="tab_planes", align_bytes=64)
         nc.vector.memset(tab_planes[:], 0)
-        nc.vector.memset(w4_plane[:], 0)
         tab_scale_words = tab_scales.bitcast(I32)
-        for q in range(QUADRANTS):
-            nc.sync.dma_start(
-                out=tab_planes[32 * q : 32 * q + SCALE_ROWS * PASSES, :],
-                in_=tab_scale_words[:, SCALE_ROWS * q : SCALE_ROWS * (q + 1), :],
-            )
-        gains = held.tile([P, PACK], F32, name="gains")
-        nc.scalar.dma_start(out=gains[:], in_=gain.rearrange("(p t) -> p t", t=PACK))
-
-        tab = []
-        for a in range(PASSES):
-            words = held.tile([P, T], I32, name="tab%d" % a, align_bytes=64)
-            nc.sync.dma_start(out=words[:], in_=tab_words[a].rearrange("p n i -> p (n i)").bitcast(I32))
-            tab.append(words)
-
-        w_raw = held.tile([P, PASSES * PACK, H], F32, name="w_raw")
-        centers = [held.tile([P, T], F32, name="centers%d" % t) for t in range(PACK)]
         center_rows = gT.rearrange("(p t) c -> t p c", t=PACK)
 
-        def load_w(a, c0, c1):
-            rows = w1[a * P * PACK : (a + 1) * P * PACK, :].rearrange("(p i) c -> p i c", i=PACK)
-            nc.sync.dma_start(out=w_raw[:, a * PACK : (a + 1) * PACK, c0:c1], in_=rows[:, :, c0:c1])
+        def load_tab(a, tag):
+            words = held.tile([P, T], I32, name="tab%d" % a, tag=tag, align_bytes=64)
+            nc.sync.dma_start(out=words[:], in_=tab_words[a].rearrange("p n i -> p (n i)").bitcast(I32))
+            return words
 
-        load_w(0, 0, H)
-        load_w(1, 0, H)
-        for t in (0, 1):
-            nc.sync.dma_start(out=centers[t][:], in_=center_rows[t])
-        load_w(2, 0, H // 2)
-        load_w(2, H // 2, H)
-        for t in LATE_SLOTS:
-            nc.sync.dma_start(out=centers[t][:], in_=center_rows[t])
-        w4 = held.tile([P, 2 * N], U8, name="w4", align_bytes=64)
-        nc.sync.dma_start(out=w4[:], in_=w4_words[0])
-        w4_scale_words = w4_scales[0].bitcast(I32)
-        for q in range(QUADRANTS):
-            nc.sync.dma_start(
-                out=w4_plane[32 * q : 32 * q + SCALE_ROWS, :],
-                in_=w4_scale_words[SCALE_ROWS * q : SCALE_ROWS * (q + 1), :],
-            )
+        def load_w(a, tag):
+            raw = held.tile([P, PACK, H], F32, name="w_raw%d" % a, tag=tag, align_bytes=64)
+            nc.sync.dma_start(out=raw[:], in_=w1[a * P * PACK : (a + 1) * P * PACK, :].rearrange("(p i) c -> p i c", i=PACK))
+            return raw
+
+        def load_centers(t, tag):
+            rows = held.tile([P, T], F32, name="centers%d" % t, tag=tag, align_bytes=64)
+            nc.sync.dma_start(out=rows[:], in_=center_rows[t])
+            return rows
 
         v_words = [held.tile([P, S], U32, name="v_words%d" % a, align_bytes=64) for a in range(PASSES)]
         v_planes = held.tile([P, S], U8, name="v_planes", align_bytes=64)
-        for a in range(PASSES):
-            nc.vector.tensor_copy(v_words[a][:], listed(tab[a][:].bitcast(U32), 0, S))
-        nc.vector.tensor_copy(v_planes[:], listed(tab_planes[:].bitcast(U8), 0, S))
-
-        w_grouped = [held.tile([P, PACK * H], BF16, name="w_grouped%d" % i, align_bytes=64) for i in range(2)]
-        w_codes = [
-            held.tile([P, H], U32, name="w_codes%d" % a, tag="planes_then_codes" if a == 0 else "w_codes%d" % a, align_bytes=64)
-            for a in range(PASSES)
-        ]
+        w_codes = [held.tile([P, H], U32, name="w_codes%d" % a, align_bytes=64) for a in range(PASSES)]
         w_planes = [held.tile([P, H], U8, name="w_plane%d" % a, align_bytes=64) for a in range(PASSES)]
 
-        def quantize_w(a, shares):
-            grouped = w_grouped[a % 2]
-            src = w_raw[:, a * PACK : (a + 1) * PACK, :].rearrange("p i (m t) -> p m i t", t=PACK)
+        def gather_words(a, words):
+            nc.vector.tensor_copy(v_words[a][:], listed(words[:].bitcast(U32), 0, S))
+
+        def quantize_w(a, raw, on_scalar):
+            grouped = held.tile([P, PACK * H], BF16, name="w_grouped%d" % a, tag="grouped%d" % (a % 2), align_bytes=64)
+            src = raw[:].rearrange("p i (m t) -> p m i t", t=PACK)
             dst = grouped[:].rearrange("p (t m i) -> p m i t", t=PACK, i=PACK)
-            for m0, m1, on_vector in shares:
-                if on_vector:
-                    nc.vector.tensor_copy(dst[:, m0:m1], src[:, m0:m1])
-                else:
-                    nc.scalar.copy(dst[:, m0:m1], src[:, m0:m1])
+            nc.scalar.copy(dst[:, 0:on_scalar], src[:, 0:on_scalar])
+            if on_scalar < P:
+                nc.vector.tensor_copy(dst[:, on_scalar:P], src[:, on_scalar:P])
             nc.vector.quantize_mx(out=w_codes[a][:].bitcast(FP8X4), scales=w_planes[a][:], in_=grouped[:])
 
-        work = held.tile([P, CHUNKS, 2 + PACK, CHUNK], F32, name="work")
-        d_half = held.tile([P, len(HALVES), BANK], F32, name="d_half")
-        h = held.tile([P, 2, CHUNK * PACK], BF16, name="h", align_bytes=64)
-
-        pieces = w_raw[:].rearrange("p r (b j) -> p (r b) j", j=CHUNK)
-        chunk_centers = [pieces[:, 16:18, :], pieces[:, 18:20, :], pieces[:, 0:5:4, :], pieces[:, 2:7:4, :]]
-
-        def project(acc, t, j0, j1, a):
+        def project(acc, t, j0, j1, a, start, stop):
             nc.tensor.matmul_mx(
                 out=acc,
                 lhsT=w_codes[a][:, t * P : (t + 1) * P].bitcast(FP8X4),
                 lhsT_scale=w_planes[a][:, t * P : (t + 1) * P],
                 rhs=v_words[a][:, j0:j1].bitcast(FP8X4),
                 rhs_scale=v_planes[SCALE_ROWS * a : P, j0:j1],
-                start=(a == 0),
-                stop=(a == PASSES - 1),
+                start=start,
+                stop=stop,
             )
 
-        def half_gather(u):
-            t, j0 = HALVES[u]
-            nc.vector.tensor_copy(w_raw[:, u, :], listed(centers[t][:], j0, j0 + BANK))
+        acc = [[psum.tile([P, BANK], F32, name="acc%d%d" % (t, u), tag="bank") for u in range(2)] for t in range(PACK)]
 
-        def half_gauss(u):
-            t, j0 = HALVES[u]
-            d = d_half[:, u, :]
-            c = j0 // CHUNK
-            nc.vector.tensor_tensor(d, half_acc[u][:], w_raw[:, u, :], ALU.subtract)
-            nc.scalar.activation(d, d, ACT.Square)
-            nc.scalar.activation(work[:, c : c + 2, 2 + t, :], d.rearrange("p (c j) -> p c j", j=CHUNK), ACT.Exp, scale=-1.0)
+        def project_pass(a):
+            for t, u in PROJECT_ORDER:
+                project(acc[t][u][:], t, u * BANK, (u + 1) * BANK, a, a == 0, a == PASSES - 1)
 
-        chunk_acc = {}
+        tab0 = load_tab(0, "big0")
+        tab1 = load_tab(1, "big2")
+        for q in range(QUADRANTS):
+            nc.sync.dma_start(
+                out=tab_planes[32 * q : 32 * q + SCALE_ROWS * PASSES, :],
+                in_=tab_scale_words[:, SCALE_ROWS * q : SCALE_ROWS * (q + 1), :],
+            )
+        raw0 = load_w(0, "big1")
+        raw1 = load_w(1, "big3")
+        tab2 = load_tab(2, "big4")
+        raw2 = load_w(2, "big5")
+        gains = held.tile([P, PACK], F32, name="gains")
+        nc.sync.dma_start(out=gains[:], in_=gain.rearrange("(p t) -> p t", t=PACK))
+        centers = [load_centers(t, "big%d" % (6 + t)) for t in range(PACK)]
+        gather_words(0, tab0)
+        gather_words(1, tab1)
+        nc.vector.tensor_copy(v_planes[:], listed(tab_planes[:].bitcast(U8), 0, S))
+        quantize_w(0, raw0, P)
+        project_pass(0)
+        gather_words(2, tab2)
+        quantize_w(1, raw1, P)
+        project_pass(1)
 
-        def chunk_project(c):
-            acc = psum_a.tile([P, 2, CHUNK], F32, name="acc")
-            for t in LATE_SLOTS:
-                for a in range(PASSES):
-                    project(acc[:, t - 2, :], t, c * CHUNK, (c + 1) * CHUNK, a)
-            chunk_acc[c] = acc
+        picked = [held.tile([P, BANK], F32, name="picked%d" % u) for u in range(2)]
+        work = held.tile([P, CHUNKS, PACK, CHUNK], F32, name="work")
 
-        def chunk_gather(c, t):
-            nc.vector.tensor_copy(chunk_centers[c][:, t - 2, :], listed(centers[t][:], c * CHUNK, (c + 1) * CHUNK))
+        quantize_w(2, raw2, W2_ON_SCALAR)
+        project_pass(2)
 
-        def chunk_gauss(c):
-            d = work[:, c, 0:2, :]
-            nc.vector.tensor_tensor(d, chunk_acc[c][:], chunk_centers[c], ALU.subtract)
-            nc.scalar.activation(d, d, ACT.Square)
-            nc.scalar.activation(work[:, c, 4:6, :], d, ACT.Exp, scale=-1.0)
+        w4 = w_codes[0][:].bitcast(U8)
+        nc.sync.dma_start(out=w_codes[0][:, 0 : 2 * N // 4].bitcast(I32), in_=w4_words[0].bitcast(I32))
+        w4_plane = w_codes[1][:].bitcast(U8)
+        w4_scale_words = w4_scales[0].bitcast(I32)
+        for q in range(QUADRANTS):
+            nc.sync.dma_start(
+                out=w_codes[1][32 * q : 32 * q + SCALE_ROWS, 0 : N // 4].bitcast(I32),
+                in_=w4_scale_words[SCALE_ROWS * q : SCALE_ROWS * (q + 1), :],
+            )
+
+        def gather(place, t, c0, c1):
+            nc.vector.tensor_copy(place, listed(centers[t][:], c0 * CHUNK, c1 * CHUNK))
+
+        def subtract(place, t, c0, c1):
+            u, j0 = divmod(c0 * CHUNK, BANK)
+            nc.vector.tensor_tensor(
+                work[:, c0:c1, t, :],
+                acc[t][u][:, j0 : j0 + (c1 - c0) * CHUNK].rearrange("p (c j) -> p c j", j=CHUNK),
+                place.rearrange("p (c j) -> p c j", j=CHUNK), ALU.subtract)
+
+        def bell(t, chunks):
+            for c in chunks:
+                nc.scalar.activation(work[:, c, t, :], work[:, c, t, :], ACT.Square)
+            for c in chunks:
+                nc.scalar.activation(work[:, c, t, :], work[:, c, t, :], ACT.Exp, scale=-1.0)
+            if t < PACK - 1:
+                for c in chunks:
+                    nc.scalar.activation(work[:, c, t, :], work[:, c, t, :], ACT.Copy, scale=gains[:, t : t + 1])
+
+        hs = [held.tile([P, CHUNK * PACK], BF16, name="h%d" % c, align_bytes=64) for c in range(CHUNKS)]
 
         def weigh(c):
-            nc.vector.tensor_tensor(
-                h[:, c % 2, :].rearrange("p (g i t) -> p g t i", i=RUN, t=PACK),
-                work[:, c, 2:, :].rearrange("p t (g i) -> p g t i", i=RUN),
-                gains[:].rearrange("p (g t i) -> p g t i", g=1, i=1).to_broadcast([P, CHUNK // RUN, PACK, RUN]),
-                ALU.mult,
+            last = work[:, c, PACK - 1, :]
+            nc.vector.tensor_scalar(last, last, gains[:, PACK - 1 : PACK], None, ALU.mult)
+
+        def weave(c):
+            nc.vector.tensor_copy(
+                hs[c][:].rearrange("p (g i t) -> p g t i", i=RUN, t=PACK),
+                work[:, c].rearrange("p t (g i) -> p g t i", i=RUN),
             )
 
-        def mix(half):
-            h_codes = ring.tile([P, BANK], U32, name="h_codes", align_bytes=64)
-            h_plane = ring.tile([P, BANK], U8, name="h_plane", align_bytes=64)
-            nc.vector.quantize_mx(out=h_codes[:].bitcast(FP8X4), scales=h_plane[:], in_=h[:].rearrange("p c w -> p (c w)"))
-            for n in range(N_TILES):
-                acc = psum_o.tile([P, BANK], F32, name="features")
-                nc.tensor.matmul_mx(
-                    out=acc[:],
-                    lhsT=w4[:, 2 * P * n : 2 * P * (n + 1)].bitcast(FP4X4),
-                    lhsT_scale=w4_plane[:].bitcast(U8)[:, P * n : P * (n + 1)],
-                    rhs=h_codes[:].bitcast(FP8X4),
-                    rhs_scale=h_plane[:],
-                    start=True,
-                    stop=True,
-                )
-                staged = ring.tile([P, BANK], F32, name="staged", bufs=N_TILES * S // BANK)
-                if n in TILES_ON_VECTOR[half]:
-                    nc.vector.tensor_copy(staged[:], acc[:])
+        results = {}
+
+        def mix(c):
+            h = hs[c]
+            h_codes = held.tile([P, CHUNK], U32, name="h_codes%d" % c, align_bytes=64)
+            h_plane = held.tile([P, CHUNK], U8, name="h_plane%d" % c, align_bytes=64)
+            nc.vector.quantize_mx(out=h_codes[:].bitcast(FP8X4), scales=h_plane[:], in_=h[:])
+            for b in range(N_TILES // 2):
+                res = psum.tile([P, BANK], F32, name="features", tag="bank")
+                for i in range(2):
+                    n = 2 * b + i
+                    nc.tensor.matmul_mx(
+                        out=res[:, i * CHUNK : (i + 1) * CHUNK],
+                        lhsT=w4[:, 2 * P * n : 2 * P * (n + 1)].bitcast(FP4X4),
+                        lhsT_scale=w4_plane[:, P * n : P * (n + 1)],
+                        rhs=h_codes[:].bitcast(FP8X4),
+                        rhs_scale=h_plane[:],
+                        start=True,
+                        stop=True,
+                    )
+                results[(c, b)] = res
+
+        def drain(c, on_vector, banks=(0, 1, 2)):
+            for b in banks:
+                res = results[(c, b)]
+                staged = held.tile([P, BANK], F32, name="staged%d_%d" % (c, b))
+                if b in on_vector:
+                    nc.vector.tensor_copy(staged[:], res[:])
                 else:
-                    nc.scalar.copy(staged[:], acc[:])
-                nc.sync.dma_start(out=out[P * n : P * (n + 1), half * BANK : (half + 1) * BANK], in_=staged[:])
+                    nc.scalar.copy(staged[:], res[:])
+                nc.sync.dma_start(
+                    out=out[2 * P * b : 2 * P * (b + 1), c * CHUNK : (c + 1) * CHUNK].rearrange("(i p) j -> p i j", p=P),
+                    in_=staged[:].rearrange("p (i j) -> p i j", j=CHUNK))
 
-        quantize_w(0, SCALAR_ALONE)
-        quantize_w(1, SCALAR_ALONE)
-        for u in range(len(HALVES)):
-            half_gather(u)
-        quantize_w(2, LAST_PASS_SHARES)
-        half_acc = [psum_a.tile([P, BANK], F32, name="acc") for u in range(len(HALVES))]
-        for a in range(PASSES):
-            for u in (0, 2, 1, 3):
-                t, j0 = HALVES[u]
-                project(half_acc[u][:], t, j0, j0 + BANK, a)
-
-        chunk_gather(0, 2)
-        chunk_gather(1, 2)
-        half_gauss(0)
-        chunk_project(0)
-        half_gauss(2)
-        chunk_project(1)
-        chunk_gather(0, 3)
-        chunk_gather(1, 3)
-        chunk_gauss(0)
-        half_gauss(1)
-        chunk_project(2)
-        chunk_gather(2, 2)
-        chunk_gather(2, 3)
-        chunk_gauss(1)
-        chunk_project(3)
-        half_gauss(3)
+        b0, b1 = picked[0][:], picked[1][:]
+        for t in range(2):
+            for u in range(2):
+                gather(picked[u][:], t, 2 * u, 2 * u + 2)
+            for u in range(2):
+                subtract(picked[u][:], t, 2 * u, 2 * u + 2)
+                bell(t, (2 * u, 2 * u + 1))
+        gather(b0, 2, 0, 2)
+        subtract(b0, 2, 0, 2)
+        bell(2, (0, 1))
+        places = [b1[:, 0:CHUNK], b1[:, CHUNK:BANK], work[:, 0, 0, :], work[:, 1, 0, :]]
+        for c in range(2):
+            gather(places[c], 3, c, c + 1)
+        for c in range(2):
+            subtract(places[c], 3, c, c + 1)
+            bell(3, (c,))
         weigh(0)
-        weigh(1)
-        chunk_gauss(2)
+        weave(0)
         mix(0)
-        chunk_gather(3, 3)
-        chunk_gather(3, 2)
-        chunk_gauss(3)
-        weigh(2)
-        weigh(3)
+        gather(b1, 2, 2, 4)
+        subtract(b1, 2, 2, 4)
+        weigh(1)
+        gather(places[2], 3, 2, 3)
+        subtract(places[2], 3, 2, 3)
+        weave(1)
         mix(1)
+        drain(0, (), (0,))
+        bell(2, (2, 3))
+        bell(3, (2,))
+        gather(places[3], 3, 3, 4)
+        subtract(places[3], 3, 3, 4)
+        drain(0, (), (1, 2))
+        bell(3, (3,))
+        weigh(2)
+        weave(2)
+        mix(2)
+        drain(1, ())
+        weigh(3)
+        weave(3)
+        mix(3)
+        drain(2, (2,))
+        drain(3, (0, 2))

@@ -26,7 +26,8 @@ CHUNK = 256
 CHUNKS = S // CHUNK
 N_TILES = N // P
 RUN = 2
-PROJECT_ORDER = [(t, u) for t in range(PACK) for u in range(2)]
+PROJECT_ORDER = [(t, u) for t in range(PACK) for u in range(2)][:-1]
+RESULT_BANKS = [(0, 1, 2), (3, 4, 7), (6, 0, 1), (5, 2, 3)]
 W2_ON_SCALAR = 48
 
 
@@ -34,7 +35,7 @@ def tile_list_ball_gauss_features_kernel(tc, tab_words, tab_scales, offs, w1, gT
     nc = tc.nc
     with ExitStack() as ctx:
         held = ctx.enter_context(tc.tile_pool(name="held", bufs=1))
-        psum = ctx.enter_context(tc.psum_pool(name="psum", bufs=8))
+        psum = ctx.enter_context(tc.psum_pool(name="psum", bufs=1))
 
         offsets = held.tile([P, S // 16], U16, name="offsets")
         nc.sync.dma_start(offsets[:], offs)
@@ -44,6 +45,8 @@ def tile_list_ball_gauss_features_kernel(tc, tab_words, tab_scales, offs, w1, gT
 
         tab_planes = held.tile([P, T // 4], I32, name="tab_planes", align_bytes=64)
         nc.vector.memset(tab_planes[:], 0)
+        w4_rows = held.tile([P, N // 4], I32, name="w4_rows", align_bytes=64)
+        nc.vector.memset(w4_rows[:], 0)
         tab_scale_words = tab_scales.bitcast(I32)
         center_rows = gT.rearrange("(p t) c -> t p c", t=PACK)
 
@@ -90,11 +93,11 @@ def tile_list_ball_gauss_features_kernel(tc, tab_words, tab_scales, offs, w1, gT
                 stop=stop,
             )
 
-        acc = [[psum.tile([P, BANK], F32, name="acc%d%d" % (t, u), tag="bank") for u in range(2)] for t in range(PACK)]
+        acc = {(t, u): psum.tile([P, BANK], F32, name="acc%d%d" % (t, u), tag="bank%d" % (2 * t + u)) for t, u in PROJECT_ORDER}
 
         def project_pass(a):
             for t, u in PROJECT_ORDER:
-                project(acc[t][u][:], t, u * BANK, (u + 1) * BANK, a, a == 0, a == PASSES - 1)
+                project(acc[(t, u)][:], t, u * BANK, (u + 1) * BANK, a, a == 0, a == PASSES - 1)
 
         tab0 = load_tab(0, "big0")
         tab1 = load_tab(1, "big2")
@@ -110,6 +113,16 @@ def tile_list_ball_gauss_features_kernel(tc, tab_words, tab_scales, offs, w1, gT
         gains = held.tile([P, PACK], F32, name="gains")
         nc.sync.dma_start(out=gains[:], in_=gain.rearrange("(p t) -> p t", t=PACK))
         centers = [load_centers(t, "big%d" % (6 + t)) for t in range(PACK)]
+        w4_tile = held.tile([P, 2 * N], U8, name="w4", align_bytes=64)
+        nc.sync.dma_start(out=w4_tile[:], in_=w4_words[0])
+        w4 = w4_tile[:]
+        w4_plane = w4_rows[:].bitcast(U8)
+        w4_scale_words = w4_scales[0].bitcast(I32)
+        for q in range(QUADRANTS):
+            nc.sync.dma_start(
+                out=w4_rows[32 * q : 32 * q + SCALE_ROWS, :],
+                in_=w4_scale_words[SCALE_ROWS * q : SCALE_ROWS * (q + 1), :],
+            )
         gather_words(0, tab0)
         gather_words(1, tab1)
         nc.vector.tensor_copy(v_planes[:], listed(tab_planes[:].bitcast(U8), 0, S))
@@ -125,16 +138,6 @@ def tile_list_ball_gauss_features_kernel(tc, tab_words, tab_scales, offs, w1, gT
         quantize_w(2, raw2, W2_ON_SCALAR)
         project_pass(2)
 
-        w4 = w_codes[0][:].bitcast(U8)
-        nc.sync.dma_start(out=w_codes[0][:, 0 : 2 * N // 4].bitcast(I32), in_=w4_words[0].bitcast(I32))
-        w4_plane = w_codes[1][:].bitcast(U8)
-        w4_scale_words = w4_scales[0].bitcast(I32)
-        for q in range(QUADRANTS):
-            nc.sync.dma_start(
-                out=w_codes[1][32 * q : 32 * q + SCALE_ROWS, 0 : N // 4].bitcast(I32),
-                in_=w4_scale_words[SCALE_ROWS * q : SCALE_ROWS * (q + 1), :],
-            )
-
         def gather(place, t, c0, c1):
             nc.vector.tensor_copy(place, listed(centers[t][:], c0 * CHUNK, c1 * CHUNK))
 
@@ -142,7 +145,7 @@ def tile_list_ball_gauss_features_kernel(tc, tab_words, tab_scales, offs, w1, gT
             u, j0 = divmod(c0 * CHUNK, BANK)
             nc.vector.tensor_tensor(
                 work[:, c0:c1, t, :],
-                acc[t][u][:, j0 : j0 + (c1 - c0) * CHUNK].rearrange("p (c j) -> p c j", j=CHUNK),
+                acc[(t, u)][:, j0 : j0 + (c1 - c0) * CHUNK].rearrange("p (c j) -> p c j", j=CHUNK),
                 place.rearrange("p (c j) -> p c j", j=CHUNK), ALU.subtract)
 
         def bell(t, chunks):
@@ -151,8 +154,8 @@ def tile_list_ball_gauss_features_kernel(tc, tab_words, tab_scales, offs, w1, gT
             for c in chunks:
                 nc.scalar.activation(work[:, c, t, :], work[:, c, t, :], ACT.Exp, scale=-1.0)
             if t < PACK - 1:
-                for c in chunks:
-                    nc.scalar.activation(work[:, c, t, :], work[:, c, t, :], ACT.Copy, scale=gains[:, t : t + 1])
+                both = work[:, chunks[0] : chunks[-1] + 1, t, :]
+                nc.gpsimd.tensor_scalar(both, both, gains[:, t : t + 1], 0.0, ALU.mult, ALU.add)
 
         hs = [held.tile([P, CHUNK * PACK], BF16, name="h%d" % c, align_bytes=64) for c in range(CHUNKS)]
 
@@ -167,6 +170,7 @@ def tile_list_ball_gauss_features_kernel(tc, tab_words, tab_scales, offs, w1, gT
             )
 
         results = {}
+        spare = [work[:, c, 2 * k : 2 * k + 2, :].rearrange("p s j -> p (s j)") for c in (2, 3) for k in range(2)]
 
         def mix(c):
             h = hs[c]
@@ -174,7 +178,7 @@ def tile_list_ball_gauss_features_kernel(tc, tab_words, tab_scales, offs, w1, gT
             h_plane = held.tile([P, CHUNK], U8, name="h_plane%d" % c, align_bytes=64)
             nc.vector.quantize_mx(out=h_codes[:].bitcast(FP8X4), scales=h_plane[:], in_=h[:])
             for b in range(N_TILES // 2):
-                res = psum.tile([P, BANK], F32, name="features", tag="bank")
+                res = psum.tile([P, BANK], F32, name="features", tag="bank%d" % RESULT_BANKS[c][b])
                 for i in range(2):
                     n = 2 * b + i
                     nc.tensor.matmul_mx(
@@ -191,54 +195,46 @@ def tile_list_ball_gauss_features_kernel(tc, tab_words, tab_scales, offs, w1, gT
         def drain(c, on_vector, banks=(0, 1, 2)):
             for b in banks:
                 res = results[(c, b)]
-                staged = held.tile([P, BANK], F32, name="staged%d_%d" % (c, b))
                 if b in on_vector:
-                    nc.vector.tensor_copy(staged[:], res[:])
+                    staged = spare.pop()
+                    nc.vector.tensor_copy(staged, res[:])
                 else:
-                    nc.scalar.copy(staged[:], res[:])
+                    staged = held.tile([P, BANK], F32, name="staged%d_%d" % (c, b))[:]
+                    nc.scalar.copy(staged, res[:])
                 nc.sync.dma_start(
                     out=out[2 * P * b : 2 * P * (b + 1), c * CHUNK : (c + 1) * CHUNK].rearrange("(i p) j -> p i j", p=P),
-                    in_=staged[:].rearrange("p (i j) -> p i j", j=CHUNK))
+                    in_=staged.rearrange("p (i j) -> p i j", j=CHUNK))
 
-        b0, b1 = picked[0][:], picked[1][:]
-        for t in range(2):
+        for t in range(3):
             for u in range(2):
                 gather(picked[u][:], t, 2 * u, 2 * u + 2)
             for u in range(2):
                 subtract(picked[u][:], t, 2 * u, 2 * u + 2)
                 bell(t, (2 * u, 2 * u + 1))
-        gather(b0, 2, 0, 2)
-        subtract(b0, 2, 0, 2)
-        bell(2, (0, 1))
-        places = [b1[:, 0:CHUNK], b1[:, CHUNK:BANK], work[:, 0, 0, :], work[:, 1, 0, :]]
-        for c in range(2):
+        acc[(3, 1)] = psum.tile([P, BANK], F32, name="acc31", tag="bank5")
+        for a in range(PASSES):
+            project(acc[(3, 1)][:], 3, BANK, S, a, a == 0, a == PASSES - 1)
+        places = [picked[0][:, 0:CHUNK], picked[0][:, CHUNK:BANK], picked[0][:, 0:CHUNK], work[:, 0, 0, :]]
+
+        def last_slot(c):
             gather(places[c], 3, c, c + 1)
-        for c in range(2):
             subtract(places[c], 3, c, c + 1)
             bell(3, (c,))
-        weigh(0)
-        weave(0)
-        mix(0)
-        gather(b1, 2, 2, 4)
-        subtract(b1, 2, 2, 4)
-        weigh(1)
-        gather(places[2], 3, 2, 3)
-        subtract(places[2], 3, 2, 3)
-        weave(1)
-        mix(1)
-        drain(0, (), (0,))
-        bell(2, (2, 3))
-        bell(3, (2,))
-        gather(places[3], 3, 3, 4)
-        subtract(places[3], 3, 3, 4)
-        drain(0, (), (1, 2))
-        bell(3, (3,))
-        weigh(2)
-        weave(2)
-        mix(2)
+
+        def finish(c):
+            weigh(c)
+            weave(c)
+            mix(c)
+
+        last_slot(0)
+        last_slot(1)
+        finish(0)
+        last_slot(2)
+        finish(1)
+        last_slot(3)
+        drain(0, ())
+        finish(2)
+        finish(3)
         drain(1, ())
-        weigh(3)
-        weave(3)
-        mix(3)
-        drain(2, (2,))
+        drain(2, (0, 1))
         drain(3, (0, 2))

@@ -26,8 +26,8 @@ CHUNK = 256
 CHUNKS = S // CHUNK
 N_TILES = N // P
 RUN = 2
-PROJECT_ORDER = [(t, u) for t in range(PACK) for u in range(2)][:-1]
-RESULT_BANKS = [(0, 1, 2), (3, 4, 7), (6, 0, 1), (5, 2, 3)]
+PROJECT_ORDER = [(0, 1), (0, 0), (1, 1), (2, 1), (1, 0), (2, 0), (3, 0)]
+RESULT_BANKS = [(0, 1, 2), (3, 5, 7), (6, 0, 1), (4, 2, 3)]
 W2_ON_SCALAR = 48
 
 
@@ -132,7 +132,7 @@ def tile_list_ball_gauss_features_kernel(tc, tab_words, tab_scales, offs, w1, gT
         quantize_w(1, raw1, P)
         project_pass(1)
 
-        picked = [held.tile([P, BANK], F32, name="picked%d" % u) for u in range(2)]
+        picked = {(t, u): held.tile([P, BANK], F32, name="picked%d%d" % (t, u)) for t in range(PACK) for u in range(2) if t < 3 or u == 0}
         work = held.tile([P, CHUNKS, PACK, CHUNK], F32, name="work")
 
         quantize_w(2, raw2, W2_ON_SCALAR)
@@ -206,35 +206,42 @@ def tile_list_ball_gauss_features_kernel(tc, tab_words, tab_scales, offs, w1, gT
                     in_=staged.rearrange("p (i j) -> p i j", j=CHUNK))
 
         for t in range(3):
+            nc.scalar.copy(work[:, 2:4, t, :], acc[(t, 1)][:].rearrange("p (c j) -> p c j", j=CHUNK))
+        for t in range(3):
             for u in range(2):
-                gather(picked[u][:], t, 2 * u, 2 * u + 2)
-            for u in range(2):
-                subtract(picked[u][:], t, 2 * u, 2 * u + 2)
-                bell(t, (2 * u, 2 * u + 1))
-        acc[(3, 1)] = psum.tile([P, BANK], F32, name="acc31", tag="bank5")
+                gather(picked[(t, u)][:], t, 2 * u, 2 * u + 2)
+            subtract(picked[(t, 0)][:], t, 0, 2)
+            bell(t, (0, 1))
+            d = work[:, 2:4, t, :]
+            nc.gpsimd.tensor_tensor(d, d, picked[(t, 1)][:].rearrange("p (c j) -> p c j", j=CHUNK), ALU.subtract)
+            bell(t, (2, 3))
+        acc[(3, 1)] = psum.tile([P, BANK], F32, name="acc31", tag="bank4")
         for a in range(PASSES):
             project(acc[(3, 1)][:], 3, BANK, S, a, a == 0, a == PASSES - 1)
-        places = [picked[0][:, 0:CHUNK], picked[0][:, CHUNK:BANK], picked[0][:, 0:CHUNK], work[:, 0, 0, :]]
+        places = [picked[(3, 0)][:, 0:CHUNK], picked[(3, 0)][:, CHUNK:BANK], picked[(3, 0)][:, 0:CHUNK], hs[0][:].bitcast(F32)[:, 0:CHUNK]]
 
         def last_slot(c):
             gather(places[c], 3, c, c + 1)
             subtract(places[c], 3, c, c + 1)
-            bell(3, (c,))
 
         def finish(c):
             weigh(c)
             weave(c)
             mix(c)
 
-        last_slot(0)
-        last_slot(1)
+        for c in range(2):
+            last_slot(c)
+            bell(3, (c,))
         finish(0)
         last_slot(2)
-        finish(1)
+        bell(3, (2,))
         last_slot(3)
-        drain(0, ())
+        finish(1)
+        drain(0, (), (0,))
+        bell(3, (3,))
+        drain(0, (), (1, 2))
         finish(2)
         finish(3)
         drain(1, ())
-        drain(2, (0, 1))
+        drain(2, (1, 2))
         drain(3, (0, 2))

@@ -26,8 +26,9 @@ CHUNK = 256
 CHUNKS = S // CHUNK
 N_TILES = N // P
 RUN = 2
-PROJECT_ORDER = [(0, 1), (0, 0), (1, 1), (2, 1), (1, 0), (2, 0), (3, 0)]
-RESULT_BANKS = [(0, 1, 2), (3, 5, 7), (6, 0, 1), (4, 2, 3)]
+PROJECT_ORDER = [(0, 0), (0, 1), (1, 1), (2, 1), (1, 0), (2, 0), (3, 0)]
+SUBTRACT_ON_GPSIMD = [(0, 0), (0, 1), (1, 1), (2, 1)]
+RESULT_BANKS = [(0, 1, 2, 3, 5, 7), (6, 4, 0, 1, 2, 3)]
 W2_ON_SCALAR = 48
 
 
@@ -169,56 +170,58 @@ def tile_list_ball_gauss_features_kernel(tc, tab_words, tab_scales, offs, w1, gT
                 work[:, c].rearrange("p t (g i) -> p g t i", i=RUN),
             )
 
+        h_codes = [held.tile([P, BANK], U32, name="h_codes%d" % u, align_bytes=64) for u in range(2)]
+        h_planes = [held.tile([P, BANK], U8, name="h_plane%d" % u, align_bytes=64) for u in range(2)]
         results = {}
-        spare = [work[:, c, 2 * k : 2 * k + 2, :].rearrange("p s j -> p (s j)") for c in (2, 3) for k in range(2)]
 
-        def mix(c):
-            h = hs[c]
-            h_codes = held.tile([P, CHUNK], U32, name="h_codes%d" % c, align_bytes=64)
-            h_plane = held.tile([P, CHUNK], U8, name="h_plane%d" % c, align_bytes=64)
-            nc.vector.quantize_mx(out=h_codes[:].bitcast(FP8X4), scales=h_plane[:], in_=h[:])
-            for b in range(N_TILES // 2):
-                res = psum.tile([P, BANK], F32, name="features", tag="bank%d" % RESULT_BANKS[c][b])
-                for i in range(2):
-                    n = 2 * b + i
-                    nc.tensor.matmul_mx(
-                        out=res[:, i * CHUNK : (i + 1) * CHUNK],
-                        lhsT=w4[:, 2 * P * n : 2 * P * (n + 1)].bitcast(FP4X4),
-                        lhsT_scale=w4_plane[:, P * n : P * (n + 1)],
-                        rhs=h_codes[:].bitcast(FP8X4),
-                        rhs_scale=h_plane[:],
-                        start=True,
-                        stop=True,
-                    )
-                results[(c, b)] = res
+        def quantize_h(c):
+            u, j0 = divmod(c * CHUNK, BANK)
+            nc.vector.quantize_mx(
+                out=h_codes[u][:, j0 : j0 + CHUNK].bitcast(FP8X4), scales=h_planes[u][:, j0 : j0 + CHUNK], in_=hs[c][:])
 
-        def drain(c, on_vector, banks=(0, 1, 2)):
-            for b in banks:
-                res = results[(c, b)]
-                if b in on_vector:
-                    staged = spare.pop()
-                    nc.vector.tensor_copy(staged, res[:])
+        def mix(u):
+            for n in range(N_TILES):
+                res = psum.tile([P, BANK], F32, name="features", tag="bank%d" % RESULT_BANKS[u][n])
+                nc.tensor.matmul_mx(
+                    out=res[:],
+                    lhsT=w4[:, 2 * P * n : 2 * P * (n + 1)].bitcast(FP4X4),
+                    lhsT_scale=w4_plane[:, P * n : P * (n + 1)],
+                    rhs=h_codes[u][:].bitcast(FP8X4),
+                    rhs_scale=h_planes[u][:],
+                    start=True,
+                    stop=True,
+                )
+                results[(u, n)] = res
+
+        def drain(u, tiles, on_vector):
+            for n in tiles:
+                if u == 0 and n in on_vector:
+                    staged = work[:, 3, n - 3 : n - 1, :].rearrange("p s j -> p (s j)")
                 else:
-                    staged = held.tile([P, BANK], F32, name="staged%d_%d" % (c, b))[:]
-                    nc.scalar.copy(staged, res[:])
-                nc.sync.dma_start(
-                    out=out[2 * P * b : 2 * P * (b + 1), c * CHUNK : (c + 1) * CHUNK].rearrange("(i p) j -> p i j", p=P),
-                    in_=staged.rearrange("p (i j) -> p i j", j=CHUNK))
+                    staged = held.tile([P, BANK], F32, name="staged%d_%d" % (u, n))[:]
+                if n in on_vector:
+                    nc.vector.tensor_copy(staged, results[(u, n)][:])
+                else:
+                    nc.scalar.copy(staged, results[(u, n)][:])
+                nc.sync.dma_start(out=out[P * n : P * (n + 1), u * BANK : (u + 1) * BANK], in_=staged)
 
-        for t in range(3):
-            nc.scalar.copy(work[:, 2:4, t, :], acc[(t, 1)][:].rearrange("p (c j) -> p c j", j=CHUNK))
+        for t, u in SUBTRACT_ON_GPSIMD:
+            nc.scalar.copy(work[:, 2 * u : 2 * u + 2, t, :], acc[(t, u)][:].rearrange("p (c j) -> p c j", j=CHUNK))
         for t in range(3):
             for u in range(2):
                 gather(picked[(t, u)][:], t, 2 * u, 2 * u + 2)
-            subtract(picked[(t, 0)][:], t, 0, 2)
-            bell(t, (0, 1))
-            d = work[:, 2:4, t, :]
-            nc.gpsimd.tensor_tensor(d, d, picked[(t, 1)][:].rearrange("p (c j) -> p c j", j=CHUNK), ALU.subtract)
-            bell(t, (2, 3))
+            for u in range(2):
+                if (t, u) in SUBTRACT_ON_GPSIMD:
+                    d = work[:, 2 * u : 2 * u + 2, t, :]
+                    nc.gpsimd.tensor_tensor(d, d, picked[(t, u)][:].rearrange("p (c j) -> p c j", j=CHUNK), ALU.subtract)
+                else:
+                    subtract(picked[(t, u)][:], t, 2 * u, 2 * u + 2)
+                if (t, u) != (2, 1):
+                    bell(t, (2 * u, 2 * u + 1))
         acc[(3, 1)] = psum.tile([P, BANK], F32, name="acc31", tag="bank4")
         for a in range(PASSES):
             project(acc[(3, 1)][:], 3, BANK, S, a, a == 0, a == PASSES - 1)
-        places = [picked[(3, 0)][:, 0:CHUNK], picked[(3, 0)][:, CHUNK:BANK], picked[(3, 0)][:, 0:CHUNK], hs[0][:].bitcast(F32)[:, 0:CHUNK]]
+        places = [picked[(3, 0)][:, 0:CHUNK], picked[(3, 0)][:, CHUNK:BANK], picked[(3, 0)][:, 0:CHUNK], picked[(3, 0)][:, CHUNK:BANK]]
 
         def last_slot(c):
             gather(places[c], 3, c, c + 1)
@@ -227,21 +230,20 @@ def tile_list_ball_gauss_features_kernel(tc, tab_words, tab_scales, offs, w1, gT
         def finish(c):
             weigh(c)
             weave(c)
-            mix(c)
+            quantize_h(c)
 
         for c in range(2):
             last_slot(c)
             bell(3, (c,))
+        bell(2, (2, 3))
         finish(0)
-        last_slot(2)
-        bell(3, (2,))
-        last_slot(3)
         finish(1)
-        drain(0, (), (0,))
-        bell(3, (3,))
-        drain(0, (), (1, 2))
+        mix(0)
+        for c in range(2, CHUNKS):
+            last_slot(c)
+            bell(3, (c,))
         finish(2)
         finish(3)
-        drain(1, ())
-        drain(2, (1, 2))
-        drain(3, (0, 2))
+        mix(1)
+        drain(0, range(N_TILES), (3, 5))
+        drain(1, range(N_TILES), (1, 3, 5))

@@ -28,6 +28,8 @@ N_TILES = N // P
 RUN = 2
 PROJECT_ORDER = [(0, 0), (0, 1), (1, 1), (2, 1), (1, 0), (2, 0), (3, 0)]
 SUBTRACT_ON_GPSIMD = [(0, 0), (0, 1), (1, 1), (2, 1)]
+SPLIT_TILES = 4
+TILE_ORDER = [(0, 1, 2, 3, 4, 5), (0, 1, 2, 3, 4, 5)]
 RESULT_BANKS = [(0, 1, 2, 3, 5, 7), (6, 4, 0, 1, 2, 3)]
 W2_ON_SCALAR = 48
 
@@ -49,6 +51,8 @@ def tile_list_ball_gauss_features_kernel(tc, tab_words, tab_scales, offs, w1, gT
         w4_rows = held.tile([P, N // 4], I32, name="w4_rows", align_bytes=64)
         nc.vector.memset(w4_rows[:], 0)
         tab_scale_words = tab_scales.bitcast(I32)
+        gains = held.tile([P, PACK], F32, name="gains")
+        nc.scalar.dma_start(out=gains[:], in_=gain.rearrange("(p t) -> p t", t=PACK))
         center_rows = gT.rearrange("(p t) c -> t p c", t=PACK)
 
         def load_tab(a, tag):
@@ -111,8 +115,6 @@ def tile_list_ball_gauss_features_kernel(tc, tab_words, tab_scales, offs, w1, gT
         raw1 = load_w(1, "big3")
         tab2 = load_tab(2, "big4")
         raw2 = load_w(2, "big5")
-        gains = held.tile([P, PACK], F32, name="gains")
-        nc.sync.dma_start(out=gains[:], in_=gain.rearrange("(p t) -> p t", t=PACK))
         centers = [load_centers(t, "big%d" % (6 + t)) for t in range(PACK)]
         w4_tile = held.tile([P, 2 * N], U8, name="w4", align_bytes=64)
         nc.sync.dma_start(out=w4_tile[:], in_=w4_words[0])
@@ -180,8 +182,8 @@ def tile_list_ball_gauss_features_kernel(tc, tab_words, tab_scales, offs, w1, gT
                 out=h_codes[u][:, j0 : j0 + CHUNK].bitcast(FP8X4), scales=h_planes[u][:, j0 : j0 + CHUNK], in_=hs[c][:])
 
         def mix(u):
-            for n in range(N_TILES):
-                res = psum.tile([P, BANK], F32, name="features", tag="bank%d" % RESULT_BANKS[u][n])
+            for n, bank in zip(TILE_ORDER[u], RESULT_BANKS[u]):
+                res = psum.tile([P, BANK], F32, name="features", tag="bank%d" % bank)
                 nc.tensor.matmul_mx(
                     out=res[:],
                     lhsT=w4[:, 2 * P * n : 2 * P * (n + 1)].bitcast(FP4X4),
@@ -193,17 +195,18 @@ def tile_list_ball_gauss_features_kernel(tc, tab_words, tab_scales, offs, w1, gT
                 )
                 results[(u, n)] = res
 
-        def drain(u, tiles, on_vector):
-            for n in tiles:
-                if u == 0 and n in on_vector:
-                    staged = work[:, 3, n - 3 : n - 1, :].rearrange("p s j -> p (s j)")
-                else:
-                    staged = held.tile([P, BANK], F32, name="staged%d_%d" % (u, n))[:]
-                if n in on_vector:
-                    nc.vector.tensor_copy(staged, results[(u, n)][:])
-                else:
-                    nc.scalar.copy(staged, results[(u, n)][:])
-                nc.sync.dma_start(out=out[P * n : P * (n + 1), u * BANK : (u + 1) * BANK], in_=staged)
+        staged = [held.tile([P, S], F32, name="staged%d" % n) for n in range(N_TILES)]
+
+        def drain(u, n, on_vector):
+            cols = slice(u * BANK, (u + 1) * BANK)
+            if on_vector:
+                nc.vector.tensor_copy(staged[n][:, cols], results[(u, n)][:])
+            else:
+                nc.scalar.copy(staged[n][:, cols], results[(u, n)][:])
+            if n < SPLIT_TILES:
+                nc.sync.dma_start(out=out[P * n : P * (n + 1), cols], in_=staged[n][:, cols])
+            elif u == 1:
+                nc.sync.dma_start(out=out[P * n : P * (n + 1), :], in_=staged[n][:])
 
         for t, u in SUBTRACT_ON_GPSIMD:
             nc.scalar.copy(work[:, 2 * u : 2 * u + 2, t, :], acc[(t, u)][:].rearrange("p (c j) -> p c j", j=CHUNK))
@@ -245,5 +248,7 @@ def tile_list_ball_gauss_features_kernel(tc, tab_words, tab_scales, offs, w1, gT
         finish(2)
         finish(3)
         mix(1)
-        drain(0, range(N_TILES), (3, 5))
-        drain(1, range(N_TILES), (1, 3, 5))
+        for n in TILE_ORDER[0]:
+            drain(0, n, False)
+        for k, n in enumerate(TILE_ORDER[1]):
+            drain(1, n, n != 4)

@@ -245,6 +245,9 @@ def tile_list_ball_gauss_features_kernel(tc, tab_words, tab_scales, offs, w1, gT
         for c in range(2, CHUNKS):
             last_slot(c)
             bell(3, (c,))
+        warm = psum.tile([P, BANK], F32, name="warm", tag="bank4")
+        for a in range(PASSES):
+            project(warm[:], 0, 0, BANK, a, True, True)
         finish(2)
         finish(3)
         mix(1)

@@ -31,7 +31,8 @@ SUBTRACT_ON_GPSIMD = [(0, 0), (0, 1), (1, 1), (2, 1)]
 SPLIT_TILES = 4
 TILE_ORDER = [(0, 1, 2, 3, 4, 5), (0, 1, 2, 3, 4, 5)]
 RESULT_BANKS = [(0, 1, 2, 3, 5, 7), (6, 4, 0, 1, 2, 3)]
-W2_ON_SCALAR = 48
+W1_ON_SCALAR = 72
+W2_ON_SCALAR = 64
 
 
 def tile_list_ball_gauss_features_kernel(tc, tab_words, tab_scales, offs, w1, gT, gain, w4_words, w4_scales, out):
@@ -41,7 +42,6 @@ def tile_list_ball_gauss_features_kernel(tc, tab_words, tab_scales, offs, w1, gT
         psum = ctx.enter_context(tc.psum_pool(name="psum", bufs=1))
 
         offsets = held.tile([P, S // 16], U16, name="offsets")
-        nc.sync.dma_start(offsets[:], offs)
 
         def listed(window, j0, j1):
             return window.indirect(offsets[:, j0 // 16 : j1 // 16])
@@ -78,14 +78,16 @@ def tile_list_ball_gauss_features_kernel(tc, tab_words, tab_scales, offs, w1, gT
         def gather_words(a, words):
             nc.vector.tensor_copy(v_words[a][:], listed(words[:].bitcast(U32), 0, S))
 
-        def quantize_w(a, raw, on_scalar):
+        def quantize_w(a, raw, on_scalar, cuts=(0, H)):
             grouped = held.tile([P, PACK * H], BF16, name="w_grouped%d" % a, tag="grouped%d" % (a % 2), align_bytes=64)
             src = raw[:].rearrange("p i (m t) -> p m i t", t=PACK)
             dst = grouped[:].rearrange("p (t m i) -> p m i t", t=PACK, i=PACK)
             nc.scalar.copy(dst[:, 0:on_scalar], src[:, 0:on_scalar])
             if on_scalar < P:
                 nc.vector.tensor_copy(dst[:, on_scalar:P], src[:, on_scalar:P])
-            nc.vector.quantize_mx(out=w_codes[a][:].bitcast(FP8X4), scales=w_planes[a][:], in_=grouped[:])
+            for c0, c1 in zip(cuts, cuts[1:]):
+                nc.vector.quantize_mx(
+                    out=w_codes[a][:, c0:c1].bitcast(FP8X4), scales=w_planes[a][:, c0:c1], in_=grouped[:, PACK * c0 : PACK * c1])
 
         def project(acc, t, j0, j1, a, start, stop):
             nc.tensor.matmul_mx(
@@ -105,13 +107,14 @@ def tile_list_ball_gauss_features_kernel(tc, tab_words, tab_scales, offs, w1, gT
                 project(acc[(t, u)][:], t, u * BANK, (u + 1) * BANK, a, a == 0, a == PASSES - 1)
 
         tab0 = load_tab(0, "big0")
-        tab1 = load_tab(1, "big2")
+        nc.sync.dma_start(offsets[:], offs)
+        raw0 = load_w(0, "big1")
         for q in range(QUADRANTS):
             nc.sync.dma_start(
                 out=tab_planes[32 * q : 32 * q + SCALE_ROWS * PASSES, :],
                 in_=tab_scale_words[:, SCALE_ROWS * q : SCALE_ROWS * (q + 1), :],
             )
-        raw0 = load_w(0, "big1")
+        tab1 = load_tab(1, "big2")
         raw1 = load_w(1, "big3")
         tab2 = load_tab(2, "big4")
         raw2 = load_w(2, "big5")
@@ -127,18 +130,18 @@ def tile_list_ball_gauss_features_kernel(tc, tab_words, tab_scales, offs, w1, gT
                 in_=w4_scale_words[SCALE_ROWS * q : SCALE_ROWS * (q + 1), :],
             )
         gather_words(0, tab0)
-        gather_words(1, tab1)
         nc.vector.tensor_copy(v_planes[:], listed(tab_planes[:].bitcast(U8), 0, S))
         quantize_w(0, raw0, P)
         project_pass(0)
-        gather_words(2, tab2)
-        quantize_w(1, raw1, P)
+        gather_words(1, tab1)
+        quantize_w(1, raw1, W1_ON_SCALAR)
         project_pass(1)
+        gather_words(2, tab2)
 
         picked = {(t, u): held.tile([P, BANK], F32, name="picked%d%d" % (t, u)) for t in range(PACK) for u in range(2) if t < 3 or u == 0}
         work = held.tile([P, CHUNKS, PACK, CHUNK], F32, name="work")
 
-        quantize_w(2, raw2, W2_ON_SCALAR)
+        quantize_w(2, raw2, W2_ON_SCALAR, (0, P, 2 * P, H))
         project_pass(2)
 
         def gather(place, t, c0, c1):
@@ -212,9 +215,17 @@ def tile_list_ball_gauss_features_kernel(tc, tab_words, tab_scales, offs, w1, gT
             nc.scalar.copy(work[:, 2 * u : 2 * u + 2, t, :], acc[(t, u)][:].rearrange("p (c j) -> p c j", j=CHUNK))
         for t in range(3):
             for u in range(2):
-                gather(picked[(t, u)][:], t, 2 * u, 2 * u + 2)
+                if (t, u) == (0, 0):
+                    for c in range(2):
+                        place = picked[(t, u)][:, c * CHUNK : (c + 1) * CHUNK]
+                        gather(place, t, c, c + 1)
+                        nc.gpsimd.tensor_tensor(work[:, c, t, :], work[:, c, t, :], place, ALU.subtract)
+                else:
+                    gather(picked[(t, u)][:], t, 2 * u, 2 * u + 2)
             for u in range(2):
-                if (t, u) in SUBTRACT_ON_GPSIMD:
+                if (t, u) == (0, 0):
+                    pass
+                elif (t, u) in SUBTRACT_ON_GPSIMD:
                     d = work[:, 2 * u : 2 * u + 2, t, :]
                     nc.gpsimd.tensor_tensor(d, d, picked[(t, u)][:].rearrange("p (c j) -> p c j", j=CHUNK), ALU.subtract)
                 else:

@@ -25,11 +25,10 @@ BANK = 512
 CHUNK = 256
 CHUNKS = S // CHUNK
 N_TILES = N // P
-RUN = 2
+RUN = 4
 PROJECT_ORDER = [(0, 0), (0, 1), (1, 1), (2, 1), (1, 0), (2, 0), (3, 0)]
 SUBTRACT_ON_GPSIMD = [(0, 0), (0, 1), (1, 1), (2, 1)]
-SPLIT_TILES = 4
-TILE_ORDER = [(0, 1, 2, 3, 4, 5), (0, 1, 2, 3, 4, 5)]
+LEAD_BANK = 6
 RESULT_BANKS = [(0, 1, 2, 3, 5, 7), (6, 4, 0, 1, 2, 3)]
 W1_ON_SCALAR = 72
 W2_ON_SCALAR = 64
@@ -52,7 +51,6 @@ def tile_list_ball_gauss_features_kernel(tc, tab_words, tab_scales, offs, w1, gT
         nc.vector.memset(w4_rows[:], 0)
         tab_scale_words = tab_scales.bitcast(I32)
         gains = held.tile([P, PACK], F32, name="gains")
-        nc.scalar.dma_start(out=gains[:], in_=gain.rearrange("(p t) -> p t", t=PACK))
         center_rows = gT.rearrange("(p t) c -> t p c", t=PACK)
 
         def load_tab(a, tag):
@@ -118,7 +116,9 @@ def tile_list_ball_gauss_features_kernel(tc, tab_words, tab_scales, offs, w1, gT
         raw1 = load_w(1, "big3")
         tab2 = load_tab(2, "big4")
         raw2 = load_w(2, "big5")
-        centers = [load_centers(t, "big%d" % (6 + t)) for t in range(PACK)]
+        centers = [load_centers(t, "big%d" % (6 + t)) for t in range(2)]
+        nc.sync.dma_start(out=gains[:], in_=gain.rearrange("(p t) -> p t", t=PACK))
+        centers.extend(load_centers(t, "big%d" % (6 + t)) for t in range(2, PACK))
         w4_tile = held.tile([P, 2 * N], U8, name="w4", align_bytes=64)
         nc.sync.dma_start(out=w4_tile[:], in_=w4_words[0])
         w4 = w4_tile[:]
@@ -154,20 +154,24 @@ def tile_list_ball_gauss_features_kernel(tc, tab_words, tab_scales, offs, w1, gT
                 acc[(t, u)][:, j0 : j0 + (c1 - c0) * CHUNK].rearrange("p (c j) -> p c j", j=CHUNK),
                 place.rearrange("p (c j) -> p c j", j=CHUNK), ALU.subtract)
 
-        def bell(t, chunks):
+        squares = held.tile([P, 2, CHUNK], F32, name="squares")
+
+        def bell(t, chunks, in_turn=False):
+            middle = {c: squares[:, c % 2, :] if in_turn else work[:, c, t, :] for c in chunks}
             for c in chunks:
-                nc.scalar.activation(work[:, c, t, :], work[:, c, t, :], ACT.Square)
+                nc.scalar.activation(middle[c], work[:, c, t, :], ACT.Square)
             for c in chunks:
-                nc.scalar.activation(work[:, c, t, :], work[:, c, t, :], ACT.Exp, scale=-1.0)
-            if t < PACK - 1:
-                both = work[:, chunks[0] : chunks[-1] + 1, t, :]
-                nc.gpsimd.tensor_scalar(both, both, gains[:, t : t + 1], 0.0, ALU.mult, ALU.add)
+                nc.scalar.activation(work[:, c, t, :], middle[c], ACT.Exp, scale=-1.0)
+
+        def weigh_on_gpsimd(t, u):
+            both = work[:, 2 * u : 2 * u + 2, t, :]
+            nc.gpsimd.tensor_scalar(both, both, gains[:, t : t + 1], 0.0, ALU.mult, ALU.add)
 
         hs = [held.tile([P, CHUNK * PACK], BF16, name="h%d" % c, align_bytes=64) for c in range(CHUNKS)]
 
-        def weigh(c):
-            last = work[:, c, PACK - 1, :]
-            nc.vector.tensor_scalar(last, last, gains[:, PACK - 1 : PACK], None, ALU.mult)
+        def weigh(t):
+            both = work[:, 2:CHUNKS, t, :]
+            nc.vector.tensor_scalar(both, both, gains[:, t : t + 1], None, ALU.mult)
 
         def weave(c):
             nc.vector.tensor_copy(
@@ -184,32 +188,33 @@ def tile_list_ball_gauss_features_kernel(tc, tab_words, tab_scales, offs, w1, gT
             nc.vector.quantize_mx(
                 out=h_codes[u][:, j0 : j0 + CHUNK].bitcast(FP8X4), scales=h_planes[u][:, j0 : j0 + CHUNK], in_=hs[c][:])
 
-        def mix(u):
-            for n, bank in zip(TILE_ORDER[u], RESULT_BANKS[u]):
-                res = psum.tile([P, BANK], F32, name="features", tag="bank%d" % bank)
-                nc.tensor.matmul_mx(
-                    out=res[:],
-                    lhsT=w4[:, 2 * P * n : 2 * P * (n + 1)].bitcast(FP4X4),
-                    lhsT_scale=w4_plane[:, P * n : P * (n + 1)],
-                    rhs=h_codes[u][:].bitcast(FP8X4),
-                    rhs_scale=h_planes[u][:],
-                    start=True,
-                    stop=True,
-                )
-                results[(u, n)] = res
+        def mix(u, n, bank, j0, j1):
+            res = psum.tile([P, j1 - j0], F32, name="features", tag="bank%d" % bank)
+            nc.tensor.matmul_mx(
+                out=res[:],
+                lhsT=w4[:, 2 * P * n : 2 * P * (n + 1)].bitcast(FP4X4),
+                lhsT_scale=w4_plane[:, P * n : P * (n + 1)],
+                rhs=h_codes[u][:, j0:j1].bitcast(FP8X4),
+                rhs_scale=h_planes[u][:, j0:j1],
+                start=True,
+                stop=True,
+            )
+            results[(u, n, j0)] = res
 
-        staged = [held.tile([P, S], F32, name="staged%d" % n) for n in range(N_TILES)]
+        staged = [held.tile([P, 2, S], F32, name="staged%d" % k) for k in range(N_TILES // 2)]
 
-        def drain(u, n, on_vector):
-            cols = slice(u * BANK, (u + 1) * BANK)
+        def drain(u, n, j0, j1, on_vector):
+            k, i = divmod(n, 2)
+            cols = slice(u * BANK + j0, u * BANK + j1)
             if on_vector:
-                nc.vector.tensor_copy(staged[n][:, cols], results[(u, n)][:])
+                nc.vector.tensor_copy(staged[k][:, i, cols], results[(u, n, j0)][:])
             else:
-                nc.scalar.copy(staged[n][:, cols], results[(u, n)][:])
-            if n < SPLIT_TILES:
-                nc.sync.dma_start(out=out[P * n : P * (n + 1), cols], in_=staged[n][:, cols])
-            elif u == 1:
-                nc.sync.dma_start(out=out[P * n : P * (n + 1), :], in_=staged[n][:])
+                nc.scalar.copy(staged[k][:, i, cols], results[(u, n, j0)][:])
+            pair = out[2 * P * k : 2 * P * (k + 1), :].rearrange("(i p) j -> p i j", p=P)
+            if u == 0:
+                nc.sync.dma_start(out=pair[:, i, cols], in_=staged[k][:, i, cols])
+            elif i == 1:
+                nc.sync.dma_start(out=pair[:, :, cols], in_=staged[k][:, :, cols])
 
         for t, u in SUBTRACT_ON_GPSIMD:
             nc.scalar.copy(work[:, 2 * u : 2 * u + 2, t, :], acc[(t, u)][:].rearrange("p (c j) -> p c j", j=CHUNK))
@@ -232,37 +237,42 @@ def tile_list_ball_gauss_features_kernel(tc, tab_words, tab_scales, offs, w1, gT
                     subtract(picked[(t, u)][:], t, 2 * u, 2 * u + 2)
                 if (t, u) != (2, 1):
                     bell(t, (2 * u, 2 * u + 1))
+                    weigh_on_gpsimd(t, u)
         acc[(3, 1)] = psum.tile([P, BANK], F32, name="acc31", tag="bank4")
         for a in range(PASSES):
             project(acc[(3, 1)][:], 3, BANK, S, a, a == 0, a == PASSES - 1)
-        places = [picked[(3, 0)][:, 0:CHUNK], picked[(3, 0)][:, CHUNK:BANK], picked[(3, 0)][:, 0:CHUNK], picked[(3, 0)][:, CHUNK:BANK]]
-
-        def last_slot(c):
-            gather(places[c], 3, c, c + 1)
-            subtract(places[c], 3, c, c + 1)
-
-        def finish(c):
-            weigh(c)
-            weave(c)
-            quantize_h(c)
-
+        for u in range(2):
+            for i in range(2):
+                gather(picked[(3, 0)][:, i * CHUNK : (i + 1) * CHUNK], 3, 2 * u + i, 2 * u + i + 1)
+            for i in range(2):
+                subtract(picked[(3, 0)][:, i * CHUNK : (i + 1) * CHUNK], 3, 2 * u + i, 2 * u + i + 1)
+        bell(3, (0, 1), True)
         for c in range(2):
-            last_slot(c)
-            bell(3, (c,))
-        bell(2, (2, 3))
-        finish(0)
-        finish(1)
-        mix(0)
-        for c in range(2, CHUNKS):
-            last_slot(c)
-            bell(3, (c,))
+            nc.gpsimd.tensor_scalar(work[:, c, 3, :], work[:, c, 3, :], gains[:, 3:4], 0.0, ALU.mult, ALU.add)
+        bell(2, (2, 3), True)
+        bell(3, (2, 3), True)
+
+        def finish(u):
+            for c in (2 * u, 2 * u + 1):
+                weave(c)
+            for c in (2 * u, 2 * u + 1):
+                quantize_h(c)
+
         warm = psum.tile([P, BANK], F32, name="warm", tag="bank4")
         for a in range(PASSES):
             project(warm[:], 0, 0, BANK, a, True, True)
-        finish(2)
-        finish(3)
-        mix(1)
-        for n in TILE_ORDER[0]:
-            drain(0, n, False)
-        for k, n in enumerate(TILE_ORDER[1]):
-            drain(1, n, n != 4)
+        pieces = [[(0, LEAD_BANK, 0, CHUNK), (0, RESULT_BANKS[0][0], CHUNK, BANK)], [(0, RESULT_BANKS[1][0], 0, BANK)]]
+        for u in range(2):
+            pieces[u].extend((n, RESULT_BANKS[u][n], 0, BANK) for n in range(1, N_TILES))
+        finish(0)
+        for piece in pieces[0]:
+            mix(0, *piece)
+        weigh(2)
+        weigh(3)
+        finish(1)
+        for piece in pieces[1]:
+            mix(1, *piece)
+        for n, bank, j0, j1 in pieces[0]:
+            drain(0, n, j0, j1, n == N_TILES - 1)
+        for n, bank, j0, j1 in pieces[1]:
+            drain(1, n, j0, j1, n % 2 == 0)

@@ -26,10 +26,7 @@ CHUNK = 256
 CHUNKS = S // CHUNK
 N_TILES = N // P
 RUN = 4
-PROJECT_ORDER = [(0, 0), (0, 1), (1, 1), (2, 1), (1, 0), (2, 0), (3, 0)]
-SUBTRACT_ON_GPSIMD = [(0, 0), (0, 1), (1, 1), (2, 1)]
-LEAD_BANK = 6
-RESULT_BANKS = [(0, 1, 2, 3, 5, 7), (6, 4, 0, 1, 2, 3)]
+PROJECT_ORDER = [(0, 0), (0, 1), (1, 1), (2, 0), (1, 0), (3, 0), (3, 1)]
 W1_ON_SCALAR = 72
 W2_ON_SCALAR = 64
 
@@ -98,7 +95,7 @@ def tile_list_ball_gauss_features_kernel(tc, tab_words, tab_scales, offs, w1, gT
                 stop=stop,
             )
 
-        acc = {(t, u): psum.tile([P, BANK], F32, name="acc%d%d" % (t, u), tag="bank%d" % (2 * t + u)) for t, u in PROJECT_ORDER}
+        acc = {(t, u): psum.tile([P, BANK], F32, name="acc%d%d" % (t, u), tag="bank%d" % b) for b, (t, u) in enumerate(PROJECT_ORDER)}
 
         def project_pass(a):
             for t, u in PROJECT_ORDER:
@@ -138,141 +135,148 @@ def tile_list_ball_gauss_features_kernel(tc, tab_words, tab_scales, offs, w1, gT
         project_pass(1)
         gather_words(2, tab2)
 
-        picked = {(t, u): held.tile([P, BANK], F32, name="picked%d%d" % (t, u)) for t in range(PACK) for u in range(2) if t < 3 or u == 0}
-        work = held.tile([P, CHUNKS, PACK, CHUNK], F32, name="work")
-
         quantize_w(2, raw2, W2_ON_SCALAR, (0, P, 2 * P, H))
         project_pass(2)
+
+        work = [held.tile([P, PACK, BANK], F32, name="work%d" % u) for u in range(2)]
+
+        def buffer(name, width=BANK, tag=None):
+            made = held.tile([P, width], F32, name=name, tag=tag or name, align_bytes=64)
+            return made[:]
+
+        def halves(place):
+            return [place[:, i * CHUNK : (i + 1) * CHUNK] for i in range(2)]
 
         def gather(place, t, c0, c1):
             nc.vector.tensor_copy(place, listed(centers[t][:], c0 * CHUNK, c1 * CHUNK))
 
-        def subtract(place, t, c0, c1):
-            u, j0 = divmod(c0 * CHUNK, BANK)
-            nc.vector.tensor_tensor(
-                work[:, c0:c1, t, :],
-                acc[(t, u)][:, j0 : j0 + (c1 - c0) * CHUNK].rearrange("p (c j) -> p c j", j=CHUNK),
-                place.rearrange("p (c j) -> p c j", j=CHUNK), ALU.subtract)
-
-        squares = held.tile([P, 2, CHUNK], F32, name="squares")
-
-        def bell(t, chunks, in_turn=False):
-            middle = {c: squares[:, c % 2, :] if in_turn else work[:, c, t, :] for c in chunks}
-            for c in chunks:
-                nc.scalar.activation(middle[c], work[:, c, t, :], ACT.Square)
-            for c in chunks:
-                nc.scalar.activation(work[:, c, t, :], middle[c], ACT.Exp, scale=-1.0)
+        def bell(place):
+            for part in halves(place):
+                nc.scalar.activation(part, part, ACT.Square)
+            for part in halves(place):
+                nc.scalar.activation(part, part, ACT.Exp, scale=-1.0)
 
         def weigh_on_gpsimd(t, u):
-            both = work[:, 2 * u : 2 * u + 2, t, :]
-            nc.gpsimd.tensor_scalar(both, both, gains[:, t : t + 1], 0.0, ALU.mult, ALU.add)
+            nc.gpsimd.tensor_scalar(work[u][:, t, :], d[(t, u)], gains[:, t : t + 1], 0.0, ALU.mult, ALU.add)
 
-        hs = [held.tile([P, CHUNK * PACK], BF16, name="h%d" % c, align_bytes=64) for c in range(CHUNKS)]
+        def weigh(t, u):
+            nc.vector.tensor_scalar(work[u][:, t, :], d[(t, u)], gains[:, t : t + 1], None, ALU.mult)
 
-        def weigh(t):
-            both = work[:, 2:CHUNKS, t, :]
-            nc.vector.tensor_scalar(both, both, gains[:, t : t + 1], None, ALU.mult)
+        d = {(0, 0): work[0][:, 0, :], (0, 1): buffer("d01"), (1, 0): buffer("d10"), (1, 1): buffer("d11"),
+             (2, 0): work[0][:, 2, :], (2, 1): work[1][:, 2, :], (3, 0): work[0][:, 3, :], (3, 1): buffer("d31")}
+        sums = {(0, 0): d[(0, 0)], (0, 1): d[(0, 1)], (1, 1): d[(1, 1)], (2, 0): work[1][:, 0, :]}
+        for key in sums:
+            nc.scalar.copy(sums[key], acc[key][:])
 
-        def weave(c):
+        picked = {key: buffer("picked%d%d" % key) for key in ((0, 0), (0, 1), (1, 0), (1, 1))}
+        for i in range(2):
+            gather(halves(picked[(0, 0)])[i], 0, i, i + 1)
+            nc.gpsimd.tensor_tensor(halves(d[(0, 0)])[i], halves(sums[(0, 0)])[i], halves(picked[(0, 0)])[i], ALU.subtract)
+        gather(picked[(0, 1)], 0, 2, 4)
+        nc.gpsimd.tensor_tensor(d[(0, 1)], sums[(0, 1)], picked[(0, 1)], ALU.subtract)
+        bell(d[(0, 0)])
+        weigh_on_gpsimd(0, 0)
+        bell(d[(0, 1)])
+        gather(picked[(1, 0)], 1, 0, 2)
+        gather(picked[(1, 1)], 1, 2, 4)
+        nc.vector.tensor_tensor(d[(1, 0)], acc[(1, 0)][:], picked[(1, 0)], ALU.subtract)
+        nc.gpsimd.tensor_tensor(d[(1, 1)], sums[(1, 1)], picked[(1, 1)], ALU.subtract)
+        bell(d[(1, 0)])
+        bell(d[(1, 1)])
+        for i in range(2):
+            place = work[i][:, 1, 0:CHUNK]
+            gather(place, 2, i, i + 1)
+            nc.gpsimd.tensor_tensor(halves(d[(2, 0)])[i], halves(sums[(2, 0)])[i], place, ALU.subtract)
+        bell(d[(2, 0)])
+        for t, u in ((1, 0), (0, 1), (1, 1), (2, 0)):
+            weigh_on_gpsimd(t, u)
+
+        def late(t, u):
+            ring = [buffer("ring%d%d%d" % (t, u, i), CHUNK, "ring%d" % i) for i in range(2)]
+            for i in range(2):
+                gather(ring[i], t, 2 * u + i, 2 * u + i + 1)
+            for i in range(2):
+                nc.vector.tensor_tensor(halves(d[(t, u)])[i], halves(acc[(t, u)][:])[i], ring[i], ALU.subtract)
+            bell(d[(t, u)])
+
+        late(3, 0)
+        weigh_on_gpsimd(3, 0)
+        acc[(2, 1)] = psum.tile([P, BANK], F32, name="acc21", tag="bank5")
+        for a in range(PASSES):
+            project(acc[(2, 1)][:], 2, BANK, S, a, a == 0, a == PASSES - 1)
+        late(3, 1)
+        late(2, 1)
+
+        hs = {}
+
+        def weave(c, tag):
+            hs[c] = held.tile([P, CHUNK * PACK], BF16, name="h%d" % c, tag=tag, align_bytes=64)
+            u, j0 = divmod(c * CHUNK, BANK)
             nc.vector.tensor_copy(
                 hs[c][:].rearrange("p (g i t) -> p g t i", i=RUN, t=PACK),
-                work[:, c].rearrange("p t (g i) -> p g t i", i=RUN),
+                work[u][:, :, j0 : j0 + CHUNK].rearrange("p t (g i) -> p g t i", i=RUN),
             )
 
         h_codes = [held.tile([P, BANK], U32, name="h_codes%d" % u, align_bytes=64) for u in range(2)]
         h_planes = [held.tile([P, BANK], U8, name="h_plane%d" % u, align_bytes=64) for u in range(2)]
-        results = {}
 
         def quantize_h(c):
             u, j0 = divmod(c * CHUNK, BANK)
             nc.vector.quantize_mx(
                 out=h_codes[u][:, j0 : j0 + CHUNK].bitcast(FP8X4), scales=h_planes[u][:, j0 : j0 + CHUNK], in_=hs[c][:])
 
-        def mix(u, n, bank, j0, j1):
-            res = psum.tile([P, j1 - j0], F32, name="features", tag="bank%d" % bank)
-            nc.tensor.matmul_mx(
-                out=res[:],
-                lhsT=w4[:, 2 * P * n : 2 * P * (n + 1)].bitcast(FP4X4),
-                lhsT_scale=w4_plane[:, P * n : P * (n + 1)],
-                rhs=h_codes[u][:, j0:j1].bitcast(FP8X4),
-                rhs_scale=h_planes[u][:, j0:j1],
-                start=True,
-                stop=True,
-            )
-            results[(u, n, j0)] = res
+        staged = held.tile([P, N_TILES, S], F32, name="staged")
+        rows = out.rearrange("(n p) j -> p n j", p=P)
 
-        staged = [held.tile([P, 2, S], F32, name="staged%d" % k) for k in range(N_TILES // 2)]
+        def mix(bank, n0, n1, j0, j1):
+            res = psum.tile([P, n1 - n0, j1 - j0], F32, name="features", tag="bank%d" % bank)
+            u = j0 // BANK
+            for n in range(n0, n1):
+                nc.tensor.matmul_mx(
+                    out=res[:, n - n0, :],
+                    lhsT=w4[:, 2 * P * n : 2 * P * (n + 1)].bitcast(FP4X4),
+                    lhsT_scale=w4_plane[:, P * n : P * (n + 1)],
+                    rhs=h_codes[u][:, j0 - u * BANK : j1 - u * BANK].bitcast(FP8X4),
+                    rhs_scale=h_planes[u][:, j0 - u * BANK : j1 - u * BANK],
+                    start=True,
+                    stop=True,
+                )
+            return res, n0, n1, j0, j1
 
-        def drain(u, n, j0, j1, on_vector):
-            k, i = divmod(n, 2)
-            cols = slice(u * BANK + j0, u * BANK + j1)
+        def drain(piece, on_vector):
+            res, n0, n1, j0, j1 = piece
             if on_vector:
-                nc.vector.tensor_copy(staged[k][:, i, cols], results[(u, n, j0)][:])
+                nc.vector.tensor_copy(staged[:, n0:n1, j0:j1], res[:])
             else:
-                nc.scalar.copy(staged[k][:, i, cols], results[(u, n, j0)][:])
-            pair = out[2 * P * k : 2 * P * (k + 1), :].rearrange("(i p) j -> p i j", p=P)
-            if u == 0:
-                nc.sync.dma_start(out=pair[:, i, cols], in_=staged[k][:, i, cols])
-            elif i == 1:
-                nc.sync.dma_start(out=pair[:, :, cols], in_=staged[k][:, :, cols])
+                nc.scalar.copy(staged[:, n0:n1, j0:j1], res[:])
 
-        for t, u in SUBTRACT_ON_GPSIMD:
-            nc.scalar.copy(work[:, 2 * u : 2 * u + 2, t, :], acc[(t, u)][:].rearrange("p (c j) -> p c j", j=CHUNK))
-        for t in range(3):
-            for u in range(2):
-                if (t, u) == (0, 0):
-                    for c in range(2):
-                        place = picked[(t, u)][:, c * CHUNK : (c + 1) * CHUNK]
-                        gather(place, t, c, c + 1)
-                        nc.gpsimd.tensor_tensor(work[:, c, t, :], work[:, c, t, :], place, ALU.subtract)
-                else:
-                    gather(picked[(t, u)][:], t, 2 * u, 2 * u + 2)
-            for u in range(2):
-                if (t, u) == (0, 0):
-                    pass
-                elif (t, u) in SUBTRACT_ON_GPSIMD:
-                    d = work[:, 2 * u : 2 * u + 2, t, :]
-                    nc.gpsimd.tensor_tensor(d, d, picked[(t, u)][:].rearrange("p (c j) -> p c j", j=CHUNK), ALU.subtract)
-                else:
-                    subtract(picked[(t, u)][:], t, 2 * u, 2 * u + 2)
-                if (t, u) != (2, 1):
-                    bell(t, (2 * u, 2 * u + 1))
-                    weigh_on_gpsimd(t, u)
-        acc[(3, 1)] = psum.tile([P, BANK], F32, name="acc31", tag="bank4")
-        for a in range(PASSES):
-            project(acc[(3, 1)][:], 3, BANK, S, a, a == 0, a == PASSES - 1)
-        for u in range(2):
-            for i in range(2):
-                gather(picked[(3, 0)][:, i * CHUNK : (i + 1) * CHUNK], 3, 2 * u + i, 2 * u + i + 1)
-            for i in range(2):
-                subtract(picked[(3, 0)][:, i * CHUNK : (i + 1) * CHUNK], 3, 2 * u + i, 2 * u + i + 1)
-        bell(3, (0, 1), True)
-        for c in range(2):
-            nc.gpsimd.tensor_scalar(work[:, c, 3, :], work[:, c, 3, :], gains[:, 3:4], 0.0, ALU.mult, ALU.add)
-        bell(2, (2, 3), True)
-        bell(3, (2, 3), True)
+        def store(n0, n1, j0, j1):
+            nc.sync.dma_start(out=rows[:, n0:n1, j0:j1], in_=staged[:, n0:n1, j0:j1])
 
-        def finish(u):
-            for c in (2 * u, 2 * u + 1):
-                weave(c)
-            for c in (2 * u, 2 * u + 1):
-                quantize_h(c)
-
-        warm = psum.tile([P, BANK], F32, name="warm", tag="bank4")
-        for a in range(PASSES):
+        for a, bank in enumerate((6, 5, 5)):
+            if a < 2:
+                warm = psum.tile([P, BANK], F32, name="warm", tag="bank%d" % bank)
             project(warm[:], 0, 0, BANK, a, True, True)
-        pieces = [[(0, LEAD_BANK, 0, CHUNK), (0, RESULT_BANKS[0][0], CHUNK, BANK)], [(0, RESULT_BANKS[1][0], 0, BANK)]]
-        for u in range(2):
-            pieces[u].extend((n, RESULT_BANKS[u][n], 0, BANK) for n in range(1, N_TILES))
-        finish(0)
-        for piece in pieces[0]:
-            mix(0, *piece)
-        weigh(2)
-        weigh(3)
-        finish(1)
-        for piece in pieces[1]:
-            mix(1, *piece)
-        for n, bank, j0, j1 in pieces[0]:
-            drain(0, n, j0, j1, n == N_TILES - 1)
-        for n, bank, j0, j1 in pieces[1]:
-            drain(1, n, j0, j1, n % 2 == 0)
+
+        weave(0, "ring0")
+        weigh(3, 1)
+        quantize_h(0)
+        first = [mix(7, 0, 1, 0, CHUNK), mix(6, 1, 2, 0, CHUNK), mix(0, 2, 4, 0, CHUNK), mix(1, 4, 6, 0, CHUNK)]
+        weave(1, "d31")
+        weigh(2, 1)
+        quantize_h(1)
+        second = [mix(2 + k, 2 * k, 2 * k + 2, CHUNK, BANK) for k in range(3)]
+        weave(2, "h2")
+        weave(3, "h3")
+        quantize_h(2)
+        quantize_h(3)
+        for piece in first + second[:2]:
+            drain(piece, False)
+            store(*piece[1:])
+        drain(second[2], True)
+        store(*second[2][1:])
+        third = [mix(bank, n, n + 1, BANK, S) for n, bank in enumerate((5, 7, 6, 0, 1, 2))]
+        for n, piece in enumerate(third):
+            drain(piece, n % 2 == 1)
+            if n % 2 == 1:
+                store(n - 1, n + 1, BANK, S)

from contextlib import ExitStack

import concourse.mybir as mybir

K, H, N, T, S = 1536, 512, 768, 2048, 1024
FLOPS = 2 * K * H * S + 2 * H * N * S

F32 = mybir.dt.float32
BF16 = mybir.dt.bfloat16
I32 = mybir.dt.int32
U32 = mybir.dt.uint32
U16 = mybir.dt.uint16
U8 = mybir.dt.uint8
FP8X4 = mybir.dt.float8_e4m3fn_x4
FP4X4 = mybir.dt.float4_e2m1fn_x4
ACT = mybir.ActivationFunctionType
ALU = mybir.AluOpType

P = 128
PACK = 4
PASSES = K // (P * PACK)
QUADRANTS = 4
SCALE_ROWS = 4
BANK = 512
CHUNK = 256
CHUNKS = S // CHUNK
N_TILES = N // P
RUN = 4
PROJECT_ORDER = [(0, 0), (0, 1), (1, 1), (2, 0), (1, 0), (3, 0), (3, 1)]
W1_ON_SCALAR = 72
W2_ON_SCALAR = 64


def tile_list_ball_gauss_features_kernel(tc, tab_words, tab_scales, offs, w1, gT, gain, w4_words, w4_scales, out):
    nc = tc.nc
    with ExitStack() as ctx:
        held = ctx.enter_context(tc.tile_pool(name="held", bufs=1))
        psum = ctx.enter_context(tc.psum_pool(name="psum", bufs=1))

        offsets = held.tile([P, S // 16], U16, name="offsets")

        def listed(window, j0, j1):
            return window.indirect(offsets[:, j0 // 16 : j1 // 16])

        tab_planes = held.tile([P, T // 4], I32, name="tab_planes", align_bytes=64)
        nc.vector.memset(tab_planes[:], 0)
        w4_rows = held.tile([P, N // 4], I32, name="w4_rows", align_bytes=64)
        nc.vector.memset(w4_rows[:], 0)
        tab_scale_words = tab_scales.bitcast(I32)
        gains = held.tile([P, PACK], F32, name="gains")
        center_rows = gT.rearrange("(p t) c -> t p c", t=PACK)

        def load_tab(a, tag):
            words = held.tile([P, T], I32, name="tab%d" % a, tag=tag, align_bytes=64)
            nc.sync.dma_start(out=words[:], in_=tab_words[a].rearrange("p n i -> p (n i)").bitcast(I32))
            return words

        def load_w(a, tag):
            raw = held.tile([P, PACK, H], F32, name="w_raw%d" % a, tag=tag, align_bytes=64)
            nc.sync.dma_start(out=raw[:], in_=w1[a * P * PACK : (a + 1) * P * PACK, :].rearrange("(p i) c -> p i c", i=PACK))
            return raw

        def load_centers(t, tag):
            rows = held.tile([P, T], F32, name="centers%d" % t, tag=tag, align_bytes=64)
            nc.sync.dma_start(out=rows[:], in_=center_rows[t])
            return rows

        v_words = [held.tile([P, S], U32, name="v_words%d" % a, align_bytes=64) for a in range(PASSES)]
        v_planes = held.tile([P, S], U8, name="v_planes", align_bytes=64)
        w_codes = [held.tile([P, H], U32, name="w_codes%d" % a, align_bytes=64) for a in range(PASSES)]
        w_planes = [held.tile([P, H], U8, name="w_plane%d" % a, align_bytes=64) for a in range(PASSES)]

        def gather_words(a, words):
            nc.vector.tensor_copy(v_words[a][:], listed(words[:].bitcast(U32), 0, S))

        def quantize_w(a, raw, on_scalar, cuts=(0, H)):
            grouped = held.tile([P, PACK * H], BF16, name="w_grouped%d" % a, tag="grouped%d" % (a % 2), align_bytes=64)
            src = raw[:].rearrange("p i (m t) -> p m i t", t=PACK)
            dst = grouped[:].rearrange("p (t m i) -> p m i t", t=PACK, i=PACK)
            nc.scalar.copy(dst[:, 0:on_scalar], src[:, 0:on_scalar])
            if on_scalar < P:
                nc.vector.tensor_copy(dst[:, on_scalar:P], src[:, on_scalar:P])
            for c0, c1 in zip(cuts, cuts[1:]):
                nc.vector.quantize_mx(
                    out=w_codes[a][:, c0:c1].bitcast(FP8X4), scales=w_planes[a][:, c0:c1], in_=grouped[:, PACK * c0 : PACK * c1])

        def project(acc, t, j0, j1, a, start, stop):
            nc.tensor.matmul_mx(
                out=acc,
                lhsT=w_codes[a][:, t * P : (t + 1) * P].bitcast(FP8X4),
                lhsT_scale=w_planes[a][:, t * P : (t + 1) * P],
                rhs=v_words[a][:, j0:j1].bitcast(FP8X4),
                rhs_scale=v_planes[SCALE_ROWS * a : P, j0:j1],
                start=start,
                stop=stop,
            )

        acc = {(t, u): psum.tile([P, BANK], F32, name="acc%d%d" % (t, u), tag="bank%d" % b) for b, (t, u) in enumerate(PROJECT_ORDER)}

        def project_pass(a):
            for t, u in PROJECT_ORDER:
                project(acc[(t, u)][:], t, u * BANK, (u + 1) * BANK, a, a == 0, a == PASSES - 1)

        tab0 = load_tab(0, "big0")
        nc.sync.dma_start(offsets[:], offs)
        raw0 = load_w(0, "big1")
        for q in range(QUADRANTS):
            nc.sync.dma_start(
                out=tab_planes[32 * q : 32 * q + SCALE_ROWS * PASSES, :],
                in_=tab_scale_words[:, SCALE_ROWS * q : SCALE_ROWS * (q + 1), :],
            )
        tab1 = load_tab(1, "big2")
        raw1 = load_w(1, "big3")
        tab2 = load_tab(2, "big4")
        raw2 = load_w(2, "big5")
        centers = [load_centers(t, "big%d" % (6 + t)) for t in range(2)]
        nc.sync.dma_start(out=gains[:], in_=gain.rearrange("(p t) -> p t", t=PACK))
        centers.extend(load_centers(t, "big%d" % (6 + t)) for t in range(2, PACK))
        w4_tile = held.tile([P, 2 * N], U8, name="w4", align_bytes=64)
        nc.sync.dma_start(out=w4_tile[:], in_=w4_words[0])
        w4 = w4_tile[:]
        w4_plane = w4_rows[:].bitcast(U8)
        w4_scale_words = w4_scales[0].bitcast(I32)
        for q in range(QUADRANTS):
            nc.sync.dma_start(
                out=w4_rows[32 * q : 32 * q + SCALE_ROWS, :],
                in_=w4_scale_words[SCALE_ROWS * q : SCALE_ROWS * (q + 1), :],
            )
        gather_words(0, tab0)
        nc.vector.tensor_copy(v_planes[:], listed(tab_planes[:].bitcast(U8), 0, S))
        quantize_w(0, raw0, P)
        project_pass(0)
        gather_words(1, tab1)
        quantize_w(1, raw1, W1_ON_SCALAR)
        project_pass(1)
        gather_words(2, tab2)

        quantize_w(2, raw2, W2_ON_SCALAR, (0, P, 2 * P, H))
        project_pass(2)

        work = [held.tile([P, PACK, BANK], F32, name="work%d" % u) for u in range(2)]

        def buffer(name, width=BANK, tag=None):
            made = held.tile([P, width], F32, name=name, tag=tag or name, align_bytes=64)
            return made[:]

        def halves(place):
            return [place[:, i * CHUNK : (i + 1) * CHUNK] for i in range(2)]

        def gather(place, t, c0, c1):
            nc.vector.tensor_copy(place, listed(centers[t][:], c0 * CHUNK, c1 * CHUNK))

        def bell(place):
            for part in halves(place):
                nc.scalar.activation(part, part, ACT.Square)
            for part in halves(place):
                nc.scalar.activation(part, part, ACT.Exp, scale=-1.0)

        def weigh_on_gpsimd(t, u):
            nc.gpsimd.tensor_scalar(work[u][:, t, :], d[(t, u)], gains[:, t : t + 1], 0.0, ALU.mult, ALU.add)

        def weigh(t, u):
            nc.vector.tensor_scalar(work[u][:, t, :], d[(t, u)], gains[:, t : t + 1], None, ALU.mult)

        d = {(0, 0): work[0][:, 0, :], (0, 1): buffer("d01"), (1, 0): buffer("d10"), (1, 1): buffer("d11"),
             (2, 0): work[0][:, 2, :], (2, 1): work[1][:, 2, :], (3, 0): work[0][:, 3, :], (3, 1): buffer("d31")}
        sums = {(0, 0): d[(0, 0)], (0, 1): d[(0, 1)], (1, 1): d[(1, 1)], (2, 0): work[1][:, 0, :]}
        for key in sums:
            nc.scalar.copy(sums[key], acc[key][:])

        picked = {key: buffer("picked%d%d" % key) for key in ((0, 0), (0, 1), (1, 0), (1, 1))}
        for i in range(2):
            gather(halves(picked[(0, 0)])[i], 0, i, i + 1)
            nc.gpsimd.tensor_tensor(halves(d[(0, 0)])[i], halves(sums[(0, 0)])[i], halves(picked[(0, 0)])[i], ALU.subtract)
        gather(picked[(0, 1)], 0, 2, 4)
        nc.gpsimd.tensor_tensor(d[(0, 1)], sums[(0, 1)], picked[(0, 1)], ALU.subtract)
        bell(d[(0, 0)])
        weigh_on_gpsimd(0, 0)
        bell(d[(0, 1)])
        gather(picked[(1, 0)], 1, 0, 2)
        gather(picked[(1, 1)], 1, 2, 4)
        nc.vector.tensor_tensor(d[(1, 0)], acc[(1, 0)][:], picked[(1, 0)], ALU.subtract)
        nc.gpsimd.tensor_tensor(d[(1, 1)], sums[(1, 1)], picked[(1, 1)], ALU.subtract)
        bell(d[(1, 0)])
        bell(d[(1, 1)])
        for i in range(2):
            place = work[i][:, 1, 0:CHUNK]
            gather(place, 2, i, i + 1)
            nc.gpsimd.tensor_tensor(halves(d[(2, 0)])[i], halves(sums[(2, 0)])[i], place, ALU.subtract)
        bell(d[(2, 0)])
        for t, u in ((1, 0), (0, 1), (1, 1), (2, 0)):
            weigh_on_gpsimd(t, u)

        def late(t, u):
            ring = [buffer("ring%d%d%d" % (t, u, i), CHUNK, "ring%d" % i) for i in range(2)]
            for i in range(2):
                gather(ring[i], t, 2 * u + i, 2 * u + i + 1)
            for i in range(2):
                nc.vector.tensor_tensor(halves(d[(t, u)])[i], halves(acc[(t, u)][:])[i], ring[i], ALU.subtract)
            bell(d[(t, u)])

        late(3, 0)
        weigh_on_gpsimd(3, 0)
        acc[(2, 1)] = psum.tile([P, BANK], F32, name="acc21", tag="bank5")
        for a in range(PASSES):
            project(acc[(2, 1)][:], 2, BANK, S, a, a == 0, a == PASSES - 1)
        late(3, 1)
        late(2, 1)

        hs = {}

        def weave(c, tag):
            hs[c] = held.tile([P, CHUNK * PACK], BF16, name="h%d" % c, tag=tag, align_bytes=64)
            u, j0 = divmod(c * CHUNK, BANK)
            nc.vector.tensor_copy(
                hs[c][:].rearrange("p (g i t) -> p g t i", i=RUN, t=PACK),
                work[u][:, :, j0 : j0 + CHUNK].rearrange("p t (g i) -> p g t i", i=RUN),
            )

        h_codes = [held.tile([P, BANK], U32, name="h_codes%d" % u, align_bytes=64) for u in range(2)]
        h_planes = [held.tile([P, BANK], U8, name="h_plane%d" % u, align_bytes=64) for u in range(2)]

        def quantize_h(c):
            u, j0 = divmod(c * CHUNK, BANK)
            nc.vector.quantize_mx(
                out=h_codes[u][:, j0 : j0 + CHUNK].bitcast(FP8X4), scales=h_planes[u][:, j0 : j0 + CHUNK], in_=hs[c][:])

        staged = held.tile([P, N_TILES, S], F32, name="staged")
        rows = out.rearrange("(n p) j -> p n j", p=P)

        def mix(bank, n0, n1, j0, j1):
            res = psum.tile([P, n1 - n0, j1 - j0], F32, name="features", tag="bank%d" % bank)
            u = j0 // BANK
            for n in range(n0, n1):
                nc.tensor.matmul_mx(
                    out=res[:, n - n0, :],
                    lhsT=w4[:, 2 * P * n : 2 * P * (n + 1)].bitcast(FP4X4),
                    lhsT_scale=w4_plane[:, P * n : P * (n + 1)],
                    rhs=h_codes[u][:, j0 - u * BANK : j1 - u * BANK].bitcast(FP8X4),
                    rhs_scale=h_planes[u][:, j0 - u * BANK : j1 - u * BANK],
                    start=True,
                    stop=True,
                )
            return res, n0, n1, j0, j1

        def drain(piece, on_vector):
            res, n0, n1, j0, j1 = piece
            if on_vector:
                nc.vector.tensor_copy(staged[:, n0:n1, j0:j1], res[:])
            else:
                nc.scalar.copy(staged[:, n0:n1, j0:j1], res[:])

        def store(n0, n1, j0, j1):
            nc.sync.dma_start(out=rows[:, n0:n1, j0:j1], in_=staged[:, n0:n1, j0:j1])

        for a, bank in enumerate((6, 5, 5)):
            if a < 2:
                warm = psum.tile([P, BANK], F32, name="warm", tag="bank%d" % bank)
            project(warm[:], 0, 0, BANK, a, True, True)

        weave(0, "ring0")
        weigh(3, 1)
        quantize_h(0)
        first = [mix(7, 0, 1, 0, CHUNK), mix(6, 1, 2, 0, CHUNK), mix(0, 2, 4, 0, CHUNK), mix(1, 4, 6, 0, CHUNK)]
        weave(1, "d31")
        weigh(2, 1)
        quantize_h(1)
        second = [mix(2 + k, 2 * k, 2 * k + 2, CHUNK, BANK) for k in range(3)]
        weave(2, "h2")
        weave(3, "h3")
        quantize_h(2)
        quantize_h(3)
        for piece in first + second[:2]:
            drain(piece, False)
            store(*piece[1:])
        drain(second[2], True)
        store(*second[2][1:])
        third = [mix(bank, n, n + 1, BANK, S) for n, bank in enumerate((5, 7, 6, 0, 1, 2))]
        for n, piece in enumerate(third):
            drain(piece, n % 2 == 1)
            if n % 2 == 1:
                store(n - 1, n + 1, BANK, S)
